import numpy as np, ml_dtypes
CORES = [6,15,38,47]
N = 4
import mx_ref
BF = ml_dtypes.bfloat16
def gentries(a):
    return np.ascontiguousarray(a.reshape(8, 16, -1).transpose(0, 2, 1)).reshape(8, -1)
def gtable(e):
    e = np.asarray(e); return np.ascontiguousarray(e.reshape(8, -1, 16).transpose(0, 2, 1)).reshape(128, -1).astype(np.int32)
def gcols(t, e):
    v = np.concatenate([t.reshape(8, 16, -1, 4), np.zeros((8, 16, 1, 4), BF)], axis=2)
    return np.ascontiguousarray(np.stack([v[g][:, e[g]] for g in range(8)])).reshape(128, -1)
def tile(rs):
    return np.stack(rs, axis=2).reshape(128, -1).astype(BF)
def cut(t, i, w=512):
    return t[:, w * i:w * i + w]
def pick(q, e):
    c = np.concatenate([q[0].reshape(128, -1, 4), np.zeros((128, 1, 4), np.uint8)], axis=1); s = np.concatenate([q[1], np.ones((16, 1), np.uint8)], axis=1)
    return (np.ascontiguousarray(c[:, e].reshape(128, -1)), np.ascontiguousarray(s[:, e]))
def join(*qs):
    return (np.concatenate([q[0] for q in qs], axis=1), np.concatenate([q[1] for q in qs], axis=1))
def put(q, e, v):
    c, s = q[0].reshape(128, -1, 4).copy(), q[1].copy(); c[:, e] = v[0].reshape(128, -1, 4); s[:, e] = v[1]
    return (c.reshape(128, -1), s)
def pk(c, s):
    return (np.ascontiguousarray(c), mx_ref.live(s))
def emit(q):
    return q[0], q[1]
def packed(v, rng):
    q = [mx_ref.quantize(np.ascontiguousarray(v[r])) for r in range(N)]
    return np.stack([a for a, b in q]), np.stack([mx_ref.plane(b, rng) for a, b in q])
def values_of_codes():
    e, c = np.zeros((128, 128, 4), np.float32), np.zeros((128, 2, 4), np.uint8)
    e[np.arange(128), np.arange(128), 0] = 1
    c[:127, :, 0] = np.arange(256).reshape(2, 128).T[:127]
    return mx_ref.matmul(mx_ref.quantize(e.reshape(128, 512).astype(BF)), (c.reshape(128, 8), np.full((16, 2), 127, np.uint8))).T.reshape(-1).astype(np.float64)
CODE_VALUE, SCALE_VALUE = values_of_codes(), 2.0 ** (np.arange(256) - 127.0)
def decode(q):
    return (CODE_VALUE[q[0]].reshape(16, 8, -1, 4) * SCALE_VALUE[q[1]][:, None, :, None] + 0.0).reshape(128, -1).astype(np.float32)
def f(rng, *shape):
    return mx_ref.flush((rng.standard_normal(shape, dtype=np.float32) * np.exp2(rng.integers(-2, 3, shape[:-1] + (1,)))).astype(BF))
def wide(rng, *shape, cols=0):
    v = rng.standard_normal(shape, dtype=np.float32) * np.exp2(rng.integers(-12, 13, shape)).astype(np.float32)
    if cols: v *= np.repeat(np.exp2(rng.integers(-cols, cols + 1, shape[:-2] + (1, shape[-1] // 4))) * (rng.random(shape[:-2] + (1, shape[-1] // 4)) > 0.0625), 4, axis=-1).astype(np.float32)
    return mx_ref.flush(v.astype(BF))
C, K, R = 448, 256, 3
def trim(v):
    v = np.array(v, dtype=np.float32)
    v[np.abs(v) < np.float32(2.0 ** -16)] = 0
    return v.astype(BF)
def stored(t):
    return np.stack([gtable(e) for e in t])
def numbers_of(rng):
    return {"x": trim(f(rng, N, 128, 4 * C)), "tg": stored(rng.integers(0, C, (N, 8, C))), "u": np.array(f(rng, N, 128, 512)), "v": np.array(f(rng, N, 128, 512))}
def weights(rng, w):
    c, p = packed(w, rng)
    return {"wc": c, "ws": p}
def keeping(rng, n):
    w = trim(f(rng, N, 128, 2048)).reshape(N, 8, 16, 4, 8, 16, 4)
    w[:, :, :n] = 0
    w[:, :, :, :, :, :n] = 0
    w = w.reshape(N, 128, 4, 128, 4)
    i = np.flatnonzero(np.arange(128) % 16 < n)
    for b in range(4): w[:, i, b, i, b] = 32
    return weights(rng, w.reshape(N, 128, 2048))
def signs(rng):
    return np.stack([rng.permutation(8) % 2 * 2.0 - 1.0 for r in range(N)])
def sizes(rng):
    return np.where(rng.permutation(N) < N // 2, 2.0 ** -30, 1.0).astype(np.float32)
def marked(rng, fire, late, t):
    d = numbers_of(rng)
    k = sizes(rng)
    x = d["x"].astype(np.float32).reshape(N, 8, 16, C, 4)
    x[:, :, :8] = rng.integers(8, 14, (N, 8, 8, C, 4))
    x[:, :, 0, :, 0] = 8 + (fire > 0)
    x[:, :, 0, :, 1] = 8 + (fire < 0)
    x[:, :, 1, :, 0] = 8 + (late > 0)
    x[:, :, 1, :, 1] = 8 + (late < 0)
    x[:, :, :8] *= k[:, None, None, None, None]
    u = d["u"].reshape(N, 128, 128, 4)
    for h in range(0, 128, 16):
        for i in (h, h + 1):
            u[:, :, i] = 0
            u[:, i, i, 0] = k.astype(BF)
            u[:, i, i, 1] = (-k).astype(BF)
    return {"x": x.reshape(N, 128, 4 * C).astype(BF), "tg": stored(t), "u": u.reshape(N, 128, 512), "v": d["v"], **keeping(rng, 8)}
def setup_inputs(rng):
    return {**numbers_of(rng), **weights(rng, trim(f(rng, N, 128, 2048)))}
def setup_inputs_counts(rng):
    o = rng.permutation(N)
    fire = -rng.integers(0, 2, (N, 8, C))
    late = rng.integers(-1, 2, (N, 8, C))
    t = rng.integers(0, C, (N, 8, C))
    for r in range(N):
        n = rng.permutation([K, K, K - 1, K + 1, C, 1, 0, K // 2])
        if o[r] == 0: n[:] = 0
        if o[r] == 1: n[:] = C
        for g in range(8): fire[r, g, rng.permutation(C)[:n[g]]] = 1
        a = rng.permutation(8)
        late[r, a[0]] = 1
        late[r, a[1]] = 0
        t[r, a[2]] = rng.integers(C)
        t[r, a[3]] = np.arange(C)
        t[r, a[4]] = np.arange(C) // 2
    return marked(rng, fire, late, t)
def setup_inputs_waves(rng):
    n = min(K, C // 2) // 4 * 4
    h = n // 2
    p = np.argsort(rng.random((N, 8, C)), axis=2)
    i = np.arange(C)
    z = n + np.where(i < h, i // 2, np.where(i < n, i, h + (i - n) % h))
    fire = -rng.integers(0, 2, (N, 8, C))
    late = -rng.integers(0, 2, (N, 8, C))
    t = np.zeros((N, 8, C), np.int64)
    np.put_along_axis(t, p, np.roll(p, -1, axis=0)[:, :, z], axis=2)
    np.put_along_axis(fire, p[:, :, :n], 1, axis=2)
    np.put_along_axis(late, p[:, :, h:n], 1, axis=2)
    return marked(rng, fire, late, t)
def setup_inputs_near(rng):
    d = numbers_of(rng)
    p = rng.permutation(C)
    back = np.argsort(p)
    s = p // 2
    way = 1 - s % 2 * 2
    digit = ((s[:, None] >> np.arange(8)) & 1) * np.exp2(np.arange(8) - 22.0)
    x = np.zeros((N, 8, 16, C, 4), np.float32)
    x[:, :, 0, :, 0] = 1
    x[:, :, 8] = digit[:, :4]
    x[:, :, 9] = digit[:, 4:]
    x[:, :, 10:] = rng.integers(4, 8, (N, 8, 6, C, 4)) * rng.choice([-1.0, 1.0], (N, 8, 6, C, 4)) * 2.0 ** -19
    k, sign = sizes(rng), signs(rng)
    u = d["u"].reshape(N, 128, 128, 4)
    u[:, :, ::16] = 0
    u[:, :, 1::16] = 0
    t = rng.integers(0, C, (N, 8, C))
    for g in range(8):
        h = 16 * g
        a = (k * sign[:, g]).astype(np.float32).astype(BF)
        u[:, h, h, 0] = a
        u[:, h + 8:h + 10, h] = a[:, None, None]
        u[:, h + 10, h + 1] = k.astype(BF)[:, None]
    for r in range(N):
        a = rng.permutation(8)
        a = a[np.argsort(-sign[r, a], kind="stable")]
        for i in (0, 4):
            t[r, a[i]] = np.arange(C)
            t[r, a[i + 1]] = back[(p + way) % C]
            t[r, a[i + 2]] = back[(p - way) % C]
    return {"x": x.reshape(N, 128, 4 * C).astype(BF), "tg": stored(t), "u": u.reshape(N, 128, 512), "v": d["v"], **keeping(rng, 16)}
def setup_inputs_huge(rng):
    d = numbers_of(rng)
    o = rng.permutation(N)
    g = signs(rng)
    g[o == 0] = -1
    g[o == 1] = 1
    c = np.stack([rng.permutation(C) % 2 * 2.0 - 1.0 for r in range(N)])
    c[o < 3] = 1
    x = 2.0 ** 30 * (0.6 + 0.4 * rng.random((N, 128, C, 4))) * c[:, None, :, None]
    u = d["u"].reshape(N, 128, 128, 4)
    u[:, :, ::16] = (2.0 ** 30 * (1 - 0.25 * rng.random((N, 128, 8, 4))) * g[:, None, :, None]).astype(np.float32).astype(BF)
    return {"x": x.astype(np.float32).reshape(N, 128, 4 * C).astype(BF), "tg": d["tg"], "u": u.reshape(N, 128, 512), "v": d["v"], **keeping(rng, 16)}
def setup_inputs_spread(rng):
    d = setup_inputs(rng)
    d["x"] = trim(wide(rng, N, 128, 4 * C, cols=6))
    return d
def check_inputs(d):
    b = []
    for k in ("x", "u", "v"):
        a = np.abs(d[k].astype(np.float32))
        if not (np.isfinite(a).all() and ((a == 0) | (a >= 2.0 ** -30) & (a <= 2.0 ** 30)).all()): b.append("a value of " + k)
    if ((d["tg"] < 0) | (d["tg"] >= C)).any(): b.append("an entry of tg")
    for r in range(N):
        if ((d["wc"][r] & 127) == 127).any(): b.append("wc: a code that is no number")
        if not (np.abs(decode(pk(d["wc"][r], d["ws"][r]))) <= 2.0 ** 30).all(): b.append("a number of W")
    return b
def spreadout(m):
    return np.repeat(np.repeat(m, 16, axis=0), 4, axis=1)
def reference(x, tg, u, v, wc, ws):
    qu = [mx_ref.quantize(u[r]) for r in range(N)]
    lay = [pk(wc[r], ws[r]) for r in range(N)]
    to = [gentries(tg[r]).astype(np.int64) for r in range(N)]
    now = [x[r] for r in range(N)]
    last = [np.zeros((8, C), np.float32) for r in range(N)]
    fired = [np.zeros((8, C), bool) for r in range(N)]
    kept = [[] for r in range(N)]
    due = np.full((N, R + 2, 8, C), -1)
    lists = [None] * N
    for t in range(R + 1):
        if t > 0:
            for r in range(N):
                got = gcols(np.concatenate(kept[r], axis=1), due[r, t])
                mean = ((now[r].astype(np.float32) + got.astype(np.float32)) * np.float32(0.5)).astype(BF)
                now[r] = np.where(spreadout(due[r, t] >= 0), np.where(spreadout(fired[r]), mean, got), now[r])
        if t == R: break
        sent, target, delay = [], [], []
        for r in range(N):
            s = mx_ref.matmul(qu[r], mx_ref.quantize(now[r])) + np.float32(0.0)
            rise = s[::16] > last[r]
            last[r] = s[::16]
            e = np.argsort(~rise, axis=1, kind="stable")[:, :K]
            e = np.where(np.take_along_axis(rise, e, axis=1), e, -1)
            m = np.zeros((8, C + 1), bool)
            np.put_along_axis(m, np.where(e < 0, C, e), True, axis=1)
            fired[r] = m[:, :C]
            q = mx_ref.quantize(gcols(now[r], e))
            h = tile([np.maximum(mx_ref.matmul(pick(lay[r], np.arange(128 * b, 128 * b + 128)), q), np.float32(0.0)) * np.float32(0.03125) for b in range(4)])
            sent.append(mx_ref.quantize(h))
            some = np.maximum(e, 0)
            target.append(np.take_along_axis(to[r], some, axis=1))
            delay.append(np.where(e < 0, 0, 1 + (np.take_along_axis(s[1::16], some, axis=1) > 0)))
            lists[r] = e
        came = decode(join(*sent)).astype(BF)
        for r in range(N):
            n = (r + 1) % N
            kept[n].append(cut(came, r, 4 * K))
            for w in (1, 2):
                for g in range(8):
                    k = np.flatnonzero(delay[r][g] == w)[::-1]
                    new = np.full(C, -1)
                    new[target[r][g, k]] = K * t + k
                    due[n, t + w, g] = np.where(due[n, t + w, g] < 0, new, due[n, t + w, g])
    y, ol = np.zeros((N, 128, C), np.float32), np.zeros((N, 8, K), np.float32)
    oc, osc = np.zeros((N, 128, 4 * C), np.uint8), np.zeros((N, 16, C), np.uint8)
    for r in range(N):
        q = mx_ref.quantize(now[r])
        y[r] = mx_ref.matmul(mx_ref.quantize(v[r]), q)
        ol[r] = lists[r]
        oc[r], osc[r] = emit(q)
    return {"y": y, "ol": ol, "oc": oc, "osc": osc}

@@ -1,0 +1,461 @@
+from concourse.mybir import dt, AluOpType, ActivationFunctionType
+
+C, K, R = 448, 256, 3
+HC = C // 2
+XO = 16
+PW = XO + C + R * K
+KO = 1104
+SL = 480
+NH = 2
+NS = 1
+F32, BF, I32, U16, U8, MX = "float32", "bfloat16", "int32", "uint16", "uint8", "float8_e4m3fn_x4"
+
+SCRATCH = {"ps": ("psum", [128, 4096], F32)}
+for _d, _bufs in (
+    (BF, {"X": 4 * C, "Xh": 4 * PW, "Bb": 4 * C, "ut": 512, "vt": 512, "one": 528, "Z": 528, "rise": C, "Rw": 480, "TT": 976, "d0": C,
+          "TK": 544, "E": 4 * K, "H": 4 * K, "tabI": 528, "sd0": C, "sdat": C, "segrow": C, "swin": 2 * SL, "ST": 2 * SL, "cont": SL,
+          "zer": 32, "maskJ": XO + C, "maskS": SL, "vm": XO + C, "vso": SL, "sc1": SL, "sc2": SL, "win0": 1376, "win1": 1376, "win2": 1376}),
+    (MX, {"xq": C, "uq": 128, "uq2": 128, "vq": 128, "wq": 512, "wl": 512, "hq": K, "cq": 512,
+          "eq0": K, "eq1": K, "eq2": K, "lq0": K, "lq1": K, "lq2": K}),
+    (U8, {"xs": C, "us": 128, "us2": 128, "vsc": 128, "wsc": 512, "wls": 512, "hs": K, "cs": 512,
+          "es0": K, "es1": K, "es2": K, "ls0": K, "ls1": K, "ls2": K}),
+    (F32, {"prev": C, "ysb": C, "olb": K, "fc": 8, "col": 16, "cols": 16, "h16": 32, "hh": 16, "lgb": 8, "Cj": 32, "c16": 32,
+           "tabF": 32, "tabM": 32, "tabB": 32, "Fr": C, "junk": C, "acc": 8, "cum": C, "val": C, "T1": C, "seg": C, "sg": 32,
+           "w1": 32, "w2": 32, "ff": 32, "sgn": 32, "vv": 32, "nfb": 32, "FB": 32, "r1": 32, "r2": 32, "r3": 32, "r4": 32, "r5": 32,
+           "Bt": 32, "mb": 32, "zs0": 32, "zs1": 32, "zs2": 32, "zl0": 32, "zl1": 32, "zl2": 32}),
+    (I32, {"pint": 8, "ci": 8, "s16": 32, "tgi": 32, "hl": 56, "a0": 32, "a1": 32, "a2": 32, "a3": 32, "a4": 32, "ib": 8, "ob": 8}),
+    (U16, {"eoff": 16, "upo": 8, "LG": 8, "LGk": 2, "rev": 16, "hlu": 56, "spos": 32, "sig": 32, "se": 8, "pos": 32, "voff": 32,
+           "oA": 32, "oB": 32}),
+):
+    for _k in _bufs:
+        SCRATCH[_k] = ("sbuf", [128, _bufs[_k]], _d)
+
+SEMAPHORES = (["sv", "sa", "st", "sp", "sent", "dtg", "du", "dx0", "dx1", "dw", "dv", "dout", "rw"]
+              + ["rc%d%d" % (_t, _h) for _t in range(R) for _h in range(NS)] + ["rl%d" % _t for _t in range(R)])
+
+
+def slot(t):
+    return XO + C + K * (R - 1 - t)
+
+
+def rank_program(g, core, T, topo):
+    rank = T.rank_of(core)
+    if rank is None:
+        return
+    n = len(T.cores)
+    dst = T.cores[(rank + 1) % n]
+    rid, pid = topo.addr(dst)[0], topo.addr(dst)[1]
+    mask = topo.mask(core, dst)
+    ne = len(topo.engines(core, dst))
+    A, AF = AluOpType, ActivationFunctionType
+
+    Q = {"v": g.vector, "a": g.scalar, "t": g.tensor, "p": g, "s": g.sync}
+    own = {"v": "sv", "a": "sa", "t": "st", "p": "sp"}
+    cnt = {}
+    known = {q: {} for q in Q}
+    log = {}
+
+    def V(name, a=0, b=None, step=1):
+        w = SCRATCH[name][1][1]
+        b = w if b is None else b
+        view = T[name][:, a:b:step] if step > 1 else T[name][:, a:b]
+        if name == "ps":
+            return (view, name, a // 512 * 512, (b + 511) // 512 * 512, 1)
+        return (view, name, a, b, step)
+
+    def meet(x, y):
+        if x[3] <= y[2] or y[3] <= x[2]:
+            return False
+        return not (x[4] == y[4] and x[4] > 1 and (x[2] - y[2]) % x[4] != 0)
+
+    def wait(q, sem, val, clock):
+        if known[q].get(sem, 0) < val:
+            Q[q].wait_ge(T.sem[sem], val)
+            known[q][sem] = val
+            for s in clock:
+                if known[q].get(s, 0) < clock[s]:
+                    known[q][s] = clock[s]
+
+    def before(q, reads, writes):
+        need = []
+        for v, wr in [(r, False) for r in reads] + [(w, True) for w in writes]:
+            for (u, uw, uq, tok) in log.get(v[1], []):
+                if (wr or uw or (v[1] == "ps" and uq != q)) and meet(u, v):
+                    need.append(tok)
+        need.sort(key=lambda k: -k[1])
+        for sem, val, clock in need:
+            wait(q, sem, val if sem in own.values() else cnt[sem], clock)
+
+    def after(q, reads, writes, sem):
+        tok = (sem, cnt[sem], dict(known[q]))
+        for v, wr in [(r, False) for r in reads] + [(w, True) for w in writes]:
+            log.setdefault(v[1], []).append((v, wr, q, tok))
+
+    def op(q, call, reads, writes):
+        before(q, reads, writes)
+        sem = own[q]
+        call().then_inc(T.sem[sem], 1)
+        cnt[sem] = cnt.get(sem, 0) + 1
+        after(q, reads, writes, sem)
+
+    def dma(q, sem, out, in_, reads, writes):
+        before(q, reads, writes)
+        Q[q].dma_start(out, in_).then_inc(T.sem[sem], 16)
+        cnt[sem] = cnt.get(sem, 0) + 16
+        after(q, reads, writes, sem)
+
+    def landed(sem, val, writes):
+        cnt[sem] = val
+        for w in writes:
+            log.setdefault(w[1], []).append((w, True, "far", (sem, val, {})))
+
+    def send(src, out, sem, codes=False):
+        before("p", [src], [])
+        a, b = (out[0].bitcast(dt.uint8), src[0].bitcast(dt.uint8)) if codes else (out[0], src[0])
+        g.remote_dma(a, b, T.sem[sem], T.sem["sent"], pid, rid, mask)
+        cnt["sent"] = cnt.get("sent", 0) + ne
+
+    def ap(x):
+        return x[0][0].indirect(x[1][0]) if len(x) == 2 else x[0]
+
+    def vs(x):
+        return [x[0], x[1]] if len(x) == 2 else [x]
+
+    def num(x):
+        return isinstance(x, (int, float)) or x is None
+
+    def ts(out, in0, s1, op0, s2=None, op1=None):
+        rd = vs(in0) + [s for s in (s1, s2) if not num(s)]
+        x1, x2 = (s1 if num(s1) else s1[0]), (s2 if num(s2) else s2[0])
+        if op1 is None:
+            op("v", lambda: g.vector.tensor_scalar(out[0], ap(in0), x1, None, op0), rd, [out])
+        else:
+            op("v", lambda: g.vector.tensor_scalar(out[0], ap(in0), x1, x2, op0, op1), rd, [out])
+
+    def tt(out, in0, in1, o):
+        op("v", lambda: g.vector.tensor_tensor(out[0], ap(in0), in1[0], o), vs(in0) + [in1], [out])
+
+    def cp(out, in_):
+        op("v", lambda: g.vector.tensor_copy(out[0], ap(in_)), vs(in_), [out])
+
+    def scatter(win, off, in_):
+        op("v", lambda: g.vector.tensor_copy(win[0].indirect(off[0]), in_[0]), [off, in_], [win])
+
+    def fill(out, c):
+        op("v", lambda: g.vector.memset(out[0], c), [], [out])
+
+    def scan(out, d0, d1, init, op0, op1):
+        rd = [d0, d1] + ([] if num(init) else [init])
+        op("v", lambda: g.vector.tensor_tensor_scan(out[0], d0[0], d1[0], init if num(init) else init[0], op0, op1), rd, [out])
+
+    def turn(out, in_):
+        op("v", lambda: g.vector.transpose(out[0], in_[0]), [in_], [out])
+
+    def act(out, in_, func=None, bias=0.0, scale=1.0, acc=None):
+        f = AF.Identity if func is None else func
+        rd = vs(in_) + [s for s in (bias, scale) if not num(s)]
+        b, s = (bias if num(bias) else bias[0]), (scale if num(scale) else scale[0])
+        if acc is None:
+            op("a", lambda: g.scalar.activation(out[0], ap(in_), f, bias=b, scale=s), rd, [out])
+        else:
+            op("a", lambda: g.scalar.activation(out[0], ap(in_), f, bias=b, scale=s, accum_out=acc[0]), rd, [out, acc])
+
+    def afill(out, c):
+        act(out, V("tabI", 0, out[3] - out[2]), scale=0.0, bias=c)
+
+    def quant(q, s, in_):
+        op("v", lambda: g.vector.quantize_mx(q[0], s[0], in_[0]), [in_], [q, s])
+
+    def mm(out, wq, ws, xq, xs):
+        op("t", lambda: g.tensor.matmul_mx(out[0], wq[0], ws[0], xq[0], xs[0], True, True), [wq, ws, xq, xs], [out])
+
+    def iota(out, pattern, base, cm, small=True):
+        if small:
+            op("p", lambda: g.iota(out[0], pattern, base, cm, allow_small_or_imprecise_dtypes=True), [], [out])
+        else:
+            op("p", lambda: g.iota(out[0], pattern, base, cm), [], [out])
+
+    def bank(b, w):
+        return V("ps", 512 * b, 512 * b + w)
+
+    def c1(name, j):
+        return V(name, j, j + 1)
+
+    def plane(t, a=0, b=PW):
+        return V("Xh", PW * t + a, PW * t + b)
+
+    spare = []
+
+    def gap(k=1):
+        for _ in range(k):
+            if spare:
+                spare.pop(0)()
+
+    dma("s", "dtg", T.tgi[:, 0:28], T.tg[:], [], [V("tgi")])
+    dma("a", "du", T.ut[:], T.u[:], [], [V("ut")])
+    for h in range(2):
+        dma("s", "dx%d" % h, T.X[:, 4 * HC * h:4 * HC * (h + 1)], T.x[:, 4 * HC * h:4 * HC * (h + 1)], [], [V("X", 4 * HC * h, 4 * HC * (h + 1))])
+    dma("s", "dw", T.wq[:].bitcast(dt.uint8), T.wc[:], [], [V("wq")])
+    dma("s", "dw", T.wsc[:], T.ws[:], [], [V("wsc")])
+    dma("s", "dv", T.vt[:], T.v[:], [], [V("vt")])
+
+    iota(c1("pint", 0), [[0, 1]], 0, 1, small=False)
+    iota(c1("pint", 1), [[0, 1]], 0, 17, small=False)
+    iota(V("hh"), [[1, 16]], 0, 0)
+    iota(V("h16"), [[16, 32]], 0, 0)
+    iota(V("lgb", 0, 6), [[1, 3], [256, 2]], 0, 0)
+    iota(V("tabI"), [[1, 528]], -256, 0)
+    iota(V("sd0"), [[32, 14], [0, 2], [1, 16]], -255, 0)
+    iota(V("s16", 0, 28), [[0, 14], [16, 2]], 0, 0, small=False)
+    fill(V("one"), 1.0)
+    op("p", lambda: g.affine_select(T.Z[:], T.one[:], [[-1, 528]], A.is_equal, 0.0, 3, 4), [V("one")], [V("Z")])
+    ts(c1("ci", 0), c1("pint", 0), 15, A.bitwise_and)
+    ts(V("ci", 1, 3), V("pint", 0, 2), 4, A.arith_shift_right, 1, A.bitwise_and)
+    fill(V("Rw"), 0.0)
+    cp(V("fc", 0, 3), V("ci", 0, 3))
+    fill(V("win0", KO - 16, 1376), -256.0)
+    fi, fs, fx = c1("fc", 0), c1("fc", 1), c1("fc", 2)
+    initc, pm = c1("col", 0), c1("col", 1)
+    d0c, i16, y, y2, k0, r16, init, f16 = [c1("cols", j) for j in range(8)]
+    ts(V("tabB", 0, 16), V("hh"), fi, A.is_lt, 1024.0, A.add)
+    ts(V("tabB", 16, 32), V("hh"), fi, A.is_lt, 1024.0, A.mult)
+    ts(V("tabF", 0, 16), V("hh"), fi, A.is_equal)
+    ts(V("tabF", 16, 32), V("hh"), fi, A.is_equal, 1024.0, A.mult)
+    ts(pm, fi, 2.0, A.not_equal)
+    ts(initc, fi, 0.0, A.is_equal, 256.0, A.mult)
+    ts(k0, fi, 1025.0, A.mult, 16384.0, A.add)
+    ts(f16, fi, float(XO), A.add)
+    act(i16, fi, scale=16.0)
+    act(r16, fs, scale=16.0)
+    act(y, fx, scale=464.0, bias=i16)
+    act(y2, fx, scale=272.0, bias=i16)
+    act(V("c16"), V("h16"), bias=f16)
+    act(V("tabM", 0, 16), V("tabF", 0, 16))
+    act(V("tabM", 16, 32), V("tabF", 0, 16), scale=2.0 ** -10)
+    ts(V("upo"), V("h16", 0, 8), pm, A.subtract, 1.0, A.add)
+    ts(d0c, initc, -4.0, A.mult, 1.0, A.add)
+    ts(V("Cj"), V("h16"), fi, A.add, float(C), A.add)
+    fill(V("Xh", XO - 1, 4 * PW, PW), 0.0)
+    fill(V("TT", 928, 976), 0.0)
+    fill(V("vm", 0, XO), 0.0)
+    fill(V("maskJ", 0, XO), 0.0)
+    ts(V("LG", 0, 6), V("lgb", 0, 6), y, A.add)
+    cp(c1("LGk", 0), y2)
+
+    hi, lo = V("hlu", 0, 28), V("hlu", 28, 56)
+    ts(V("hl", 0, 28), V("tgi", 0, 28), 4, A.arith_shift_right)
+    ts(V("hl", 28, 56), V("tgi", 0, 28), 15, A.bitwise_and)
+    quant(V("uq"), V("us"), V("ut"))
+    cp(V("hlu"), V("hl"))
+    act(V("junk"), (V("tabB"), hi), acc=c1("acc", 0))
+    act(init, c1("acc", 0), bias=k0)
+    act(V("d0"), V("tabI", 0, C), scale=0.0, bias=d0c)
+    afill(V("segrow"), 1.0)
+    act(V("segrow", 0, C, 16), V("h16", 0, 28), scale=0.0)
+    act(V("sdat"), V("sd0"), bias=r16)
+    afill(V("swin", 0, SL), -256.0)
+    afill(V("swin", SL, 2 * SL), -256.0)
+    op("v", lambda: g.vector.tensor_copy(T.uq2[:].bitcast(dt.uint32), T.uq[:].bitcast(dt.uint32).indirect(T.upo[:])), [V("uq"), V("upo")], [V("uq2")])
+    cp(V("Fr"), (V("tabF"), hi))
+    op("v", lambda: g.vector.tensor_copy(T.us2[:], T.us[:].indirect(T.upo[:])), [V("us"), V("upo")], [V("us2")])
+    scan(V("cum"), V("Fr"), V("Fr"), init, A.add, A.max)
+
+    sort_calls = [
+        lambda: tt(V("val"), (V("tabM"), hi), V("cum"), A.mult),
+        lambda: turn(V("T1"), V("val")),
+        lambda: scan(V("seg"), V("segrow"), V("T1"), 0.0, A.mult, A.add),
+        lambda: cp(V("a0", 0, 28), V("seg", 15, C, 16)),
+        lambda: (ts(V("a1", 0, 28), V("a0", 0, 28), 1023, A.bitwise_and), ts(V("a2", 0, 28), V("a0", 0, 28), 1008, A.bitwise_and)),
+        lambda: tt(V("a3", 0, 28), V("a1", 0, 28), V("s16", 0, 28), A.add),
+        lambda: tt(V("a4", 0, 28), V("a3", 0, 28), V("a2", 0, 28), A.add),
+        lambda: cp(V("spos", 0, 28), V("a4", 0, 28)),
+    ]
+
+    def sort_scatter():
+        cp(c1("ib", 0), init)
+        cp(c1("ib", 1), c1("cum", C - 1))
+        fill(V("zer"), 0.0)
+        scatter(V("swin"), V("spos", 0, 28), V("sdat"))
+        ts(V("ob", 0, 4, 2), V("ib", 0, 2), 1023, A.bitwise_and)
+        ts(V("ob", 1, 4, 2), V("ib", 0, 2), 10, A.arith_shift_right)
+
+    def sort_order():
+        turn(V("ST"), V("swin"))
+        cp(V("se", 0, 4), V("ob", 0, 4))
+        tt(V("sg", 0, 30), V("ST", 0, 2 * SL, 32), V("ST", 16, 2 * SL, 32), A.add)
+        scatter(V("cont"), V("se", 0, 2), V("zer"))
+        ts(V("sig", 0, 30), V("sg", 0, 30), 512.0 + XO - 1, A.add)
+        act(V("maskS"), (V("maskJ"), V("sig", 0, 30)))
+
+    def score(h, a, b, sq, ss):
+        q, s = V("xq", a, b), V("xs", a, b)
+        quant(q, s, V("X", 4 * a, 4 * b))
+        mm(bank(h, b - a), V(sq), V(ss), q, s)
+
+    def rises(t, h):
+        a, e = HC * h, HC * (h + 1)
+        if t == 0:
+            ts(V("rise", a, e), bank(h, HC), 0.0, A.is_gt)
+        else:
+            tt(V("rise", a, e), bank(h, HC), V("prev", a, e), A.is_gt)
+        if t < R - 1:
+            act(V("prev", a, e), bank(h, HC), scale=pm)
+
+    def count(h):
+        a, e = HC * h, HC * (h + 1)
+        scan(V("Rw", 16 + a, 16 + e), V("d0", a, e), V("rise", a, e), initc if h == 0 else c1("Rw", 15 + a), A.max, A.subtract)
+
+    def turn_a(h):
+        turn(V("TT", HC * h, HC * (h + 1)), V("Rw", 16 + HC * h, 16 + HC * (h + 1)))
+
+    def turn_b(h):
+        turn(V("TT", C + HC * h, C + HC * (h + 1) + 32 * h), V("Rw", HC * h, HC * (h + 1) + 32 * h))
+
+    def second(t):
+        rises(t, 0)
+        score(1, HC, C, "uq2", "us2")
+        count(0)
+        gap()
+        turn_a(0)
+
+    def merge(t, last):
+        lq, ls, zl = "lq%d" % t, "ls%d" % t, "zl%d" % t
+        landed("rl%d" % t, ne, [V(zl)])
+        for h in range(NS):
+            landed("rc%d%d" % (t, h), 2 * ne, [V(lq, K // NS * h, K // NS * (h + 1)), V(ls, K // NS * h, K // NS * (h + 1))])
+        w = K // NH
+        db = [[bank((2 + 4 * h + b) % 8, w) for b in range(4)] for h in range(NH)]
+        for h in range(NH):
+            a, e = w * h, w * (h + 1)
+            for b in range(4):
+                mm(db[h][b], V("wl", 128 * b, 128 * b + 128), V("wls", 128 * b, 128 * b + 128), V(lq, a, e), V(ls, a, e))
+        for h in range(NH):
+            a, e = w * h, w * (h + 1)
+            for b in range(0, 4, 2):
+                ts(V("H", 4 * a + b, 4 * e, 4), db[h][b], 0.0, A.max, 0.03125, A.mult)
+                act(V("H", 4 * a + b + 1, 4 * e, 4), db[h][b + 1], func=AF.Relu, scale=0.03125)
+            quant(V("hq", a, e), V("hs", a, e), V("H", 4 * a, 4 * e))
+            for b in range(4):
+                mm(db[h][b], V("cq", 128 * b, 128 * b + 128), V("cs", 128 * b, 128 * b + 128), V("hq", a, e), V("hs", a, e))
+        tt(V("mb"), V(zl), V("FB"), A.min)
+        cp(V("oA"), V(zl))
+        cp(V("oB"), V("mb"))
+        for h in range(NH):
+            a, e = slot(t) + w * h, slot(t) + w * (h + 1)
+            for b in range(4):
+                if b == 0 or h < NH - 1:
+                    act(plane(b, a, e), db[h][b], scale=0.5)
+                else:
+                    ts(plane(b, a, e), db[h][b], 0.5, A.mult)
+        cuts = [0, 320, C] if last else [0, HC, C]
+        for h in range(2):
+            a, e = cuts[h], cuts[h + 1]
+            for b in range(4):
+                act(V("Bb", C * b + a, C * b + e), (plane(b), V("oB", a // 16, e // 16)))
+        for h in range(2):
+            a, e = cuts[h], cuts[h + 1]
+            for b in range(4):
+                tt(V("X", 4 * a + b, 4 * e, 4), (plane(b), V("oA", a // 16, e // 16)), V("Bb", C * b + a, C * b + e), A.add)
+            if last:
+                score(h, a, e, "vq", "vsc")
+                store(h, a, e)
+            elif h == 0:
+                score(h, a, e, "uq2", "us2")
+            else:
+                second(t + 1)
+
+    def store(h, a, e):
+        dma("s", "dout", T.oc[:, 4 * a:4 * e], T.xq[:, a:e].bitcast(dt.uint8), [V("xq", a, e)], [])
+        if h == 1:
+            for k in range(4):
+                dma("sa"[k % 2], "dout", T.osc[4 * k:4 * k + 4, :], T.xs[32 * k:32 * k + 4, :], [V("xs")], [])
+        act(V("ysb", a, e), bank(h, e - a))
+        dma("a", "dout", T.y[:, a:e], T.ysb[:, a:e], [V("ysb", a, e)], [])
+
+    def fire(t):
+        win = "win%d" % t
+        for b in range(4):
+            act(plane(b, XO, XO + C), V("X", b, 4 * C, 4), scale=0.5)
+        rises(t, 1)
+        turn_b(0)
+        count(1)
+        gap()
+        turn_a(1)
+        turn_b(1)
+        if t == 0:
+            act(V("maskJ", XO, XO + C), (V("tabF", 0, 16), lo))
+            afill(V("cont"), 1.0)
+        gap()
+        tt(V("w1"), (V("TT"), V("LG", 2, 4)), V("Cj"), A.mult)
+        ts(V("sgn"), (V("TT"), V("LG", 4, 6)), 2.0, A.mult, -1.0, A.add)
+        tt(V("w2"), (V("TT"), V("LG", 0, 2)), V("w1"), A.subtract)
+        gap()
+        ts(V("pos"), V("w2"), float(KO), A.add)
+        ts(V("ff"), V("w2"), 1.0, A.add, 0.0, A.max)
+        scatter(V(win), V("pos", 0, 28), V("tabI", 1, 1 + C))
+        tt(V("vv"), V("ff"), V("sgn"), A.mult)
+        turn(V("TK", 0, K), V(win, KO, KO + K))
+        turn(V("TK", K, K + 288), V(win, KO - 16, 1376))
+        ts(V("voff"), V("vv"), 256.0, A.add)
+        ts(V("eoff"), (V("TK"), c1("LGk", 0)), 255.0 + XO, A.add)
+        ts(V("nfb"), V("w2"), -0.5, A.is_lt, 4096.0, A.mult)
+        w = K // NS
+        for h in range(NS):
+            a, e = w * h, w * (h + 1)
+            for b in range(4):
+                src = (plane(b, 0, XO + C), V("eoff", a // 16, e // 16))
+                if t == 0 or b % 2:
+                    act(V("E", 4 * a + b, 4 * e, 4), src, scale=2.0)
+                else:
+                    ts(V("E", 4 * a + b, 4 * e, 4), src, 2.0, A.mult)
+            if t == 0 and h == 0:
+                gap(len(spare))
+                sort_scatter()
+            quant(V("eq%d" % t, a, e), V("es%d" % t, a, e), V("E", 4 * a, 4 * e))
+            send(V("eq%d" % t, a, e), V("lq%d" % t, a, e), "rc%d%d" % (t, h), codes=True)
+            send(V("es%d" % t, a, e), V("ls%d" % t, a, e), "rc%d%d" % (t, h))
+        act(V("vm", XO, XO + C), (V("tabI"), V("voff", 0, 28)))
+
+    def route(t):
+        ends = V("se", 2, 4)
+        tt(V("FB"), V("nfb"), V("c16"), A.add)
+        if t < R - 1:
+            fill(V("win%d" % (t + 1), KO - 16, 1376), -256.0)
+        tt(V("vso"), (V("vm"), V("sig", 0, 30)), V("maskS"), A.mult)
+        scan(V("sc1"), V("cont"), V("vso"), 0.0, A.mult, A.max)
+        ts(V("r1"), (V("sc1"), ends), 0.0, A.is_gt, float(slot(t) - 1), A.mult)
+        tt(V("r2"), (V("sc1"), ends), V("r1"), A.add)
+        tt(V("zs%d" % t), V("r2"), V("c16" if t == 0 else "Bt"), A.max)
+        send(V("zs%d" % t), V("zl%d" % t), "rl%d" % t)
+        if t < R - 1:
+            scan(V("sc2"), V("cont"), V("vso"), 0.0, A.mult, A.min)
+            ts(V("r3"), (V("sc2"), ends), 0.0, A.is_lt, float(1 - slot(t)), A.mult)
+            tt(V("r4"), (V("sc2"), ends), V("r3"), A.add)
+            ts(V("r5"), V("r4"), -1.0, A.mult)
+            tt(V("Bt"), V("r5"), V("c16"), A.max)
+
+    send(V("wq"), V("wl"), "rw", codes=True)
+    send(V("wsc"), V("wls"), "rw")
+    landed("rw", 2 * ne, [V("wl"), V("wls")])
+    spare.extend(sort_calls)
+    gap()
+    score(0, 0, HC, "uq2", "us2")
+    gap()
+    second(0)
+    for t in range(R):
+        fire(t)
+        if t == 0:
+            sort_order()
+            for b in range(4):
+                quant(V("cq", 128 * b, 128 * b + 128), V("cs", 128 * b, 128 * b + 128), V("Z", 3 - b, 515 - b))
+        route(t)
+        if t == 1:
+            ts(V("rev"), V("c16", 0, 16), -1.0, A.mult, 255.0 + XO, A.add)
+            quant(V("vq"), V("vsc"), V("vt"))
+        if t == R - 1:
+            act(V("olb"), (V("win%d" % t, KO, KO + K), V("rev")), bias=255.0)
+            dma("s", "dout", T.ol[:], T.olb[0:128:16, :], [V("olb")], [])
+        merge(t, t == R - 1)
+
+    for sem in cnt:
+        wait("p", sem, cnt[sem], {})

@@ -2,17 +2,16 @@ from concourse.mybir import dt, AluOpType, ActivationFunctionType
 
 C, K, R = 448, 256, 3
 HC = C // 2
+HK = K // 2
 XO = 16
 PW = XO + C + R * K
 KO = 1104
 SL = 480
-NH = 2
-NS = 1
 F32, BF, I32, U16, U8, MX = "float32", "bfloat16", "int32", "uint16", "uint8", "float8_e4m3fn_x4"
 
 SCRATCH = {"ps": ("psum", [128, 4096], F32)}
 for _d, _bufs in (
-    (BF, {"X": 4 * C, "Xh": 4 * PW, "Bb": 4 * C, "ut": 512, "vt": 512, "one": 528, "Z": 528, "rise": C, "Rw": 480, "TT": 976, "d0": C,
+    (BF, {"X": 4 * C, "Xh": 8 * PW, "Bb": 4 * C, "ut": 512, "vt": 512, "one": 528, "Z": 528, "rise": C, "Rw": 480, "TT": 976, "d0": C,
           "TK": 544, "E": 4 * K, "H": 4 * K, "tabI": 528, "sd0": C, "sdat": C, "segrow": C, "swin": 2 * SL, "ST": 2 * SL, "cont": SL,
           "zer": 32, "maskJ": XO + C, "maskS": SL, "vm": XO + C, "vso": SL, "sc1": SL, "sc2": SL, "win0": 1376, "win1": 1376, "win2": 1376}),
     (MX, {"xq": C, "uq": 128, "uq2": 128, "vq": 128, "wq": 512, "wl": 512, "hq": K, "cq": 512,
@@ -31,7 +30,7 @@ for _d, _bufs in (
         SCRATCH[_k] = ("sbuf", [128, _bufs[_k]], _d)
 
 SEMAPHORES = (["sv", "sa", "st", "sp", "sent", "dtg", "du", "dx0", "dx1", "dw", "dv", "dout", "rw"]
-              + ["rc%d%d" % (_t, _h) for _t in range(R) for _h in range(NS)] + ["rl%d" % _t for _t in range(R)])
+              + ["rc%d%d" % (_t, _h) for _t in range(R) for _h in range(2)] + ["rl%d" % _t for _t in range(R)])
 
 
 def slot(t):
@@ -163,6 +162,12 @@ def rank_program(g, core, T, topo):
     def afill(out, c):
         act(out, V("tabI", 0, out[3] - out[2]), scale=0.0, bias=c)
 
+    def times(q, out, in_, c):
+        if q == "a":
+            act(out, in_, scale=c)
+        else:
+            ts(out, in_, c, A.mult)
+
     def quant(q, s, in_):
         op("v", lambda: g.vector.quantize_mx(q[0], s[0], in_[0]), [in_], [q, s])
 
@@ -181,8 +186,8 @@ def rank_program(g, core, T, topo):
     def c1(name, j):
         return V(name, j, j + 1)
 
-    def plane(t, a=0, b=PW):
-        return V("Xh", PW * t + a, PW * t + b)
+    def plane(t, a=0, b=2 * PW):
+        return V("Xh", 2 * PW * t + a, 2 * PW * t + b)
 
     spare = []
 
@@ -235,7 +240,7 @@ def rank_program(g, core, T, topo):
     ts(V("upo"), V("h16", 0, 8), pm, A.subtract, 1.0, A.add)
     ts(d0c, initc, -4.0, A.mult, 1.0, A.add)
     ts(V("Cj"), V("h16"), fi, A.add, float(C), A.add)
-    fill(V("Xh", XO - 1, 4 * PW, PW), 0.0)
+    fill(V("Xh", XO - 1, 8 * PW, 2 * PW), 0.0)
     fill(V("TT", 928, 976), 0.0)
     fill(V("vm", 0, XO), 0.0)
     fill(V("maskJ", 0, XO), 0.0)
@@ -247,6 +252,7 @@ def rank_program(g, core, T, topo):
     ts(V("hl", 28, 56), V("tgi", 0, 28), 15, A.bitwise_and)
     quant(V("uq"), V("us"), V("ut"))
     cp(V("hlu"), V("hl"))
+    op("a", lambda: g.scalar.activation(T.us2[:], T.us[:].indirect(T.upo[:]), AF.Copy), [V("us"), V("upo")], [V("us2")])
     act(V("junk"), (V("tabB"), hi), acc=c1("acc", 0))
     act(init, c1("acc", 0), bias=k0)
     act(V("d0"), V("tabI", 0, C), scale=0.0, bias=d0c)
@@ -257,10 +263,9 @@ def rank_program(g, core, T, topo):
     afill(V("swin", SL, 2 * SL), -256.0)
     op("v", lambda: g.vector.tensor_copy(T.uq2[:].bitcast(dt.uint32), T.uq[:].bitcast(dt.uint32).indirect(T.upo[:])), [V("uq"), V("upo")], [V("uq2")])
     cp(V("Fr"), (V("tabF"), hi))
-    op("v", lambda: g.vector.tensor_copy(T.us2[:], T.us[:].indirect(T.upo[:])), [V("us"), V("upo")], [V("us2")])
-    scan(V("cum"), V("Fr"), V("Fr"), init, A.add, A.max)
 
     sort_calls = [
+        lambda: scan(V("cum"), V("Fr"), V("Fr"), init, A.add, A.max),
         lambda: tt(V("val"), (V("tabM"), hi), V("cum"), A.mult),
         lambda: turn(V("T1"), V("val")),
         lambda: scan(V("seg"), V("segrow"), V("T1"), 0.0, A.mult, A.add),
@@ -287,10 +292,11 @@ def rank_program(g, core, T, topo):
         ts(V("sig", 0, 30), V("sg", 0, 30), 512.0 + XO - 1, A.add)
         act(V("maskS"), (V("maskJ"), V("sig", 0, 30)))
 
-    def score(h, a, b, sq, ss):
+    def score(h, sq, ss):
+        a, b = HC * h, HC * (h + 1)
         q, s = V("xq", a, b), V("xs", a, b)
         quant(q, s, V("X", 4 * a, 4 * b))
-        mm(bank(h, b - a), V(sq), V(ss), q, s)
+        mm(bank(h, HC), V(sq), V(ss), q, s)
 
     def rises(t, h):
         a, e = HC * h, HC * (h + 1)
@@ -313,67 +319,84 @@ def rank_program(g, core, T, topo):
 
     def second(t):
         rises(t, 0)
-        score(1, HC, C, "uq2", "us2")
+        score(1, "uq2", "us2")
         count(0)
         gap()
         turn_a(0)
 
+    def kept(h):
+        for b in range(4):
+            act(V("Bb", C * b + HC * h, C * b + HC * (h + 1)), (plane(b, 0, XO + C), V("oB", 14 * h, 14 * h + 14)))
+
     def merge(t, last):
         lq, ls, zl = "lq%d" % t, "ls%d" % t, "zl%d" % t
         landed("rl%d" % t, ne, [V(zl)])
-        for h in range(NS):
-            landed("rc%d%d" % (t, h), 2 * ne, [V(lq, K // NS * h, K // NS * (h + 1)), V(ls, K // NS * h, K // NS * (h + 1))])
-        w = K // NH
-        db = [[bank((2 + 4 * h + b) % 8, w) for b in range(4)] for h in range(NH)]
-        for h in range(NH):
-            a, e = w * h, w * (h + 1)
+        landed("rc%d0" % t, 2 * ne, [V(lq, 0, HK), V(ls)])
+        landed("rc%d1" % t, ne, [V(lq, HK, K)])
+        db = [[bank((2 + 4 * h + b) % 8, HK) for b in range(4)] for h in range(2)]
+        for h in range(2):
+            a, e = HK * h, HK * (h + 1)
             for b in range(4):
                 mm(db[h][b], V("wl", 128 * b, 128 * b + 128), V("wls", 128 * b, 128 * b + 128), V(lq, a, e), V(ls, a, e))
-        for h in range(NH):
-            a, e = w * h, w * (h + 1)
+        for h in range(2):
+            a, e = HK * h, HK * (h + 1)
             for b in range(0, 4, 2):
                 ts(V("H", 4 * a + b, 4 * e, 4), db[h][b], 0.0, A.max, 0.03125, A.mult)
                 act(V("H", 4 * a + b + 1, 4 * e, 4), db[h][b + 1], func=AF.Relu, scale=0.03125)
             quant(V("hq", a, e), V("hs", a, e), V("H", 4 * a, 4 * e))
             for b in range(4):
                 mm(db[h][b], V("cq", 128 * b, 128 * b + 128), V("cs", 128 * b, 128 * b + 128), V("hq", a, e), V("hs", a, e))
-        tt(V("mb"), V(zl), V("FB"), A.min)
-        cp(V("oA"), V(zl))
-        cp(V("oB"), V("mb"))
-        for h in range(NH):
-            a, e = slot(t) + w * h, slot(t) + w * (h + 1)
-            for b in range(4):
-                if b == 0 or h < NH - 1:
-                    act(plane(b, a, e), db[h][b], scale=0.5)
-                else:
-                    ts(plane(b, a, e), db[h][b], 0.5, A.mult)
-        cuts = [0, 320, C] if last else [0, HC, C]
-        for h in range(2):
-            a, e = cuts[h], cuts[h + 1]
-            for b in range(4):
-                act(V("Bb", C * b + a, C * b + e), (plane(b), V("oB", a // 16, e // 16)))
-        for h in range(2):
-            a, e = cuts[h], cuts[h + 1]
-            for b in range(4):
-                tt(V("X", 4 * a + b, 4 * e, 4), (plane(b), V("oA", a // 16, e // 16)), V("Bb", C * b + a, C * b + e), A.add)
-            if last:
-                score(h, a, e, "vq", "vsc")
-                store(h, a, e)
-            elif h == 0:
-                score(h, a, e, "uq2", "us2")
-            else:
-                second(t + 1)
 
-    def store(h, a, e):
+        def half(h, b, q):
+            times(q, plane(b, slot(t) + HK * h, slot(t) + HK * (h + 1)), db[h][b], 0.5)
+
+        def whole(h, b, q):
+            a, e = slot(t) + HK * h, slot(t) + HK * (h + 1)
+            times(q, plane(b, PW + a, PW + e), plane(b, a, e), 2.0)
+
+        def add(h, b):
+            a, e = HC * h, HC * (h + 1)
+            tt(V("X", 4 * a + b, 4 * e, 4), (plane(b), V("oA", 14 * h, 14 * h + 14)), V("Bb", C * b + a, C * b + e), A.add)
+
+        for b in range(4):
+            half(0, b, "a")
+        tt(V("mb"), V(zl), V("nfb"), A.add)
+        whole(0, 0, "v")
+        cp(V("oA"), V("mb"))
+        whole(0, 1, "v")
+        for b in range(4):
+            half(1, b, "va"[b % 2])
+        whole(0, 2, "v")
+        whole(1, 0, "v")
+        whole(0, 3, "a")
+        for b in range(1, 4):
+            whole(1, b, "a")
+        kept(1)
+        for b in range(4):
+            add(0, b)
+        add(1, 0)
+        score(0, "vq" if last else "uq2", "vsc" if last else "us2")
+        if last:
+            store(0)
+        for b in range(1, 4):
+            add(1, b)
+        if last:
+            score(1, "vq", "vsc")
+            store(1)
+        else:
+            second(t + 1)
+
+    def store(h):
+        a, e = HC * h, HC * (h + 1)
         dma("s", "dout", T.oc[:, 4 * a:4 * e], T.xq[:, a:e].bitcast(dt.uint8), [V("xq", a, e)], [])
         if h == 1:
             for k in range(4):
                 dma("sa"[k % 2], "dout", T.osc[4 * k:4 * k + 4, :], T.xs[32 * k:32 * k + 4, :], [V("xs")], [])
-        act(V("ysb", a, e), bank(h, e - a))
+        act(V("ysb", a, e), bank(h, HC))
         dma("a", "dout", T.y[:, a:e], T.ysb[:, a:e], [V("ysb", a, e)], [])
 
     def fire(t):
-        win = "win%d" % t
+        win, eq, es, lq = "win%d" % t, "eq%d" % t, "es%d" % t, "lq%d" % t
         for b in range(4):
             act(plane(b, XO, XO + C), V("X", b, 4 * C, 4), scale=0.5)
         rises(t, 1)
@@ -385,6 +408,9 @@ def rank_program(g, core, T, topo):
         if t == 0:
             act(V("maskJ", XO, XO + C), (V("tabF", 0, 16), lo))
             afill(V("cont"), 1.0)
+        else:
+            for b in range(4):
+                act(plane(b, PW + XO, PW + XO + C), V("X", b, 4 * C, 4))
         gap()
         tt(V("w1"), (V("TT"), V("LG", 2, 4)), V("Cj"), A.mult)
         ts(V("sgn"), (V("TT"), V("LG", 4, 6)), 2.0, A.mult, -1.0, A.add)
@@ -392,55 +418,58 @@ def rank_program(g, core, T, topo):
         gap()
         ts(V("pos"), V("w2"), float(KO), A.add)
         ts(V("ff"), V("w2"), 1.0, A.add, 0.0, A.max)
+        gap()
         scatter(V(win), V("pos", 0, 28), V("tabI", 1, 1 + C))
         tt(V("vv"), V("ff"), V("sgn"), A.mult)
         turn(V("TK", 0, K), V(win, KO, KO + K))
         turn(V("TK", K, K + 288), V(win, KO - 16, 1376))
         ts(V("voff"), V("vv"), 256.0, A.add)
         ts(V("eoff"), (V("TK"), c1("LGk", 0)), 255.0 + XO, A.add)
-        ts(V("nfb"), V("w2"), -0.5, A.is_lt, 4096.0, A.mult)
-        w = K // NS
-        for h in range(NS):
-            a, e = w * h, w * (h + 1)
+        ts(V("nfb"), V("w2"), -0.5, A.is_lt, float(PW), A.mult)
+        for h in range(2):
+            a, e = HK * h, HK * (h + 1)
             for b in range(4):
-                src = (plane(b, 0, XO + C), V("eoff", a // 16, e // 16))
-                if t == 0 or b % 2:
-                    act(V("E", 4 * a + b, 4 * e, 4), src, scale=2.0)
-                else:
-                    ts(V("E", 4 * a + b, 4 * e, 4), src, 2.0, A.mult)
+                times("a" if t == 0 or b % 2 else "v", V("E", 4 * a + b, 4 * e, 4), (plane(b, 0, XO + C), V("eoff", 8 * h, 8 * h + 8)), 2.0)
             if t == 0 and h == 0:
                 gap(len(spare))
                 sort_scatter()
-            quant(V("eq%d" % t, a, e), V("es%d" % t, a, e), V("E", 4 * a, 4 * e))
-            send(V("eq%d" % t, a, e), V("lq%d" % t, a, e), "rc%d%d" % (t, h), codes=True)
-            send(V("es%d" % t, a, e), V("ls%d" % t, a, e), "rc%d%d" % (t, h))
+            quant(V(eq, a, e), V(es, a, e), V("E", 4 * a, 4 * e))
+            if h == 1:
+                send(V(es), V("ls%d" % t), "rc%d0" % t)
+            send(V(eq, a, e), V(lq, a, e), "rc%d%d" % (t, h), codes=True)
         act(V("vm", XO, XO + C), (V("tabI"), V("voff", 0, 28)))
 
     def route(t):
         ends = V("se", 2, 4)
-        tt(V("FB"), V("nfb"), V("c16"), A.add)
+        tt(V("FB"), V("c16"), V("nfb"), A.subtract)
         if t < R - 1:
             fill(V("win%d" % (t + 1), KO - 16, 1376), -256.0)
+        ts(V("oB"), V("FB"), XO - 1.0, A.max)
         tt(V("vso"), (V("vm"), V("sig", 0, 30)), V("maskS"), A.mult)
+        kept(0)
         scan(V("sc1"), V("cont"), V("vso"), 0.0, A.mult, A.max)
         ts(V("r1"), (V("sc1"), ends), 0.0, A.is_gt, float(slot(t) - 1), A.mult)
         tt(V("r2"), (V("sc1"), ends), V("r1"), A.add)
         tt(V("zs%d" % t), V("r2"), V("c16" if t == 0 else "Bt"), A.max)
         send(V("zs%d" % t), V("zl%d" % t), "rl%d" % t)
+        if t == 0:
+            for b in range(4):
+                ts(plane(b, PW + XO, PW + XO + C), plane(b, XO, XO + C), 2.0, A.mult)
         if t < R - 1:
             scan(V("sc2"), V("cont"), V("vso"), 0.0, A.mult, A.min)
-            ts(V("r3"), (V("sc2"), ends), 0.0, A.is_lt, float(1 - slot(t)), A.mult)
-            tt(V("r4"), (V("sc2"), ends), V("r3"), A.add)
-            ts(V("r5"), V("r4"), -1.0, A.mult)
-            tt(V("Bt"), V("r5"), V("c16"), A.max)
+            spare.extend([
+                lambda: ts(V("r3"), (V("sc2"), ends), 0.0, A.is_lt, float(1 - slot(t)), A.mult),
+                lambda: tt(V("r4"), (V("sc2"), ends), V("r3"), A.add),
+                lambda: ts(V("r5"), V("r4"), -1.0, A.mult),
+                lambda: tt(V("Bt"), V("r5"), V("c16"), A.max),
+            ])
 
     send(V("wq"), V("wl"), "rw", codes=True)
     send(V("wsc"), V("wls"), "rw")
     landed("rw", 2 * ne, [V("wl"), V("wls")])
     spare.extend(sort_calls)
-    gap()
-    score(0, 0, HC, "uq2", "us2")
-    gap()
+    score(0, "uq2", "us2")
+    gap(2)
     second(0)
     for t in range(R):
         fire(t)
@@ -448,6 +477,7 @@ def rank_program(g, core, T, topo):
             sort_order()
             for b in range(4):
                 quant(V("cq", 128 * b, 128 * b + 128), V("cs", 128 * b, 128 * b + 128), V("Z", 3 - b, 515 - b))
+        gap(len(spare))
         route(t)
         if t == 1:
             ts(V("rev"), V("c16", 0, 16), -1.0, A.mult, 255.0 + XO, A.add)

@@ -4,27 +4,52 @@ C, K, R = 448, 256, 3
 HC = C // 2
 HK = K // 2
 XO = 16
-PW = XO + C + R * K
-KO = 1104
-SL = 480
+RX = 4 * C + 16
+PW = R * 4 * K
+FAR = 32768.0
+STEP = 65536.0
+ASIDE = 4096.0
+SL = 512
 F32, BF, I32, U16, U8, MX = "float32", "bfloat16", "int32", "uint16", "uint8", "float8_e4m3fn_x4"
+
+START = """
+    ih16 ihh one up0 pad mj0:v up1 ipint ci1 ci0 ms0:a fi tF0 vmz:v nil:a cu0:a icm tB0 tM1:a ijj tB1 tM0:a pre0:a tF1:v
+    lo Z cm:a hi hlu is16 acc k0:v Fr:a tiny:v isdat Qu Dg init:a us0 itabI sw0:a uq0 us1 uq1 +jt0:a kc:a nthr:a
+    QX0 cq0 segrow r16:a cum QX1 sw1:a sendW score0 val f4:a ib1 rise0 ib0 count0 T1 ob0 reach0 seg steps0:a
+    J a0 g2 sdat:a since0 a2 a1 g1 a3 big:a eoff delay0 a4 E01:a ob1 spos E02:a hc E13:a E00:a E03:a E10:a E11:a
+    scatter E12:a ST QE0 sg QE1 sig maskJ:a signed0 maskS1:a se marks0 maskS0:a Dn cq3 vso1:a +layer0 vso0:a open
+    prev0:a cq2 sc1 +relu01:a +relu02:a c64:v +layer1 +relu03:a r1 zs +relu00:v +relu11:a +relu12:a cq1 +QH0 hp
+    +relu13:a +own:v +relu10:a fr +QH1 fP:v Dp:a +Qv +half01:a +sc2 nf:a FB +half02:v +r3 +q +mb +oB0 +half10:a
+    +half00:a +mc +half03:a +oB1 +r4:v +half12:a +half13:a +oB3 +half11:a +oB2 +whole0:a +whole1:v
+    +oA1 +B01:a +oA2 +oA3 +B00:a +Bt +oA0"""
+ROUND = """
+    add01 B03:a add00 B02:a add03 B10:a B11:a add02 add10 B12:a QX0 add11 score0 add12 rise0 B13:a add13
+    count0 delay0 +own:a prev0:a QX1 score1 signed0 steps0:a rise1 reach0 delay1 since0 pre:a count1 signed1 marks0
+    reach1 steps1:a marks1 J since1 vso1:a vso0:a g2 g1 eoff
+    sc1 E02:a r1 r2 E00:a E01:v zs E03:a E11:a QE0 E10:a E12:a E13:v QE1
+    hc hp fr fP:v nf:v jt1:a +sc2 FB +layer0 +mb +q prev1:a +r4:a +oB1 +oB0 +B01:a +oB2
+    +relu01:a +mc +r3 +relu02:a +B00:v +layer1 +relu10:a +relu00:v +relu03:v +Bt +QH0 +oA1 +relu12:a +relu11:v +relu13:a +oA0 +QH1
+    +half00:a +half01:a +half03:a +half02:v +oB3 +half10:a +oA2 +half11:a +whole0:v +half12:a +half13:v +oA3 +whole1:v"""
+END = """
+    -Lu B03:a B02:a add00 B10:a add01 -ol:a add03 add02 add10 B11:a QX0 B12:a y0 add11 B13:a ys0:a add12 add13 QX1 y1 ys1:v"""
 
 SCRATCH = {"ps": ("psum", [128, 4096], F32)}
 for _d, _bufs in (
-    (BF, {"X": 4 * C, "Xh": 8 * PW, "Bb": 4 * C, "ut": 512, "vt": 512, "one": 528, "Z": 528, "rise": C, "Rw": 480, "TT": 976, "d0": C,
-          "TK": 544, "E": 4 * K, "H": 4 * K, "tabI": 528, "sd0": C, "sdat": C, "segrow": C, "swin": 2 * SL, "ST": 2 * SL, "cont": SL,
-          "zer": 32, "maskJ": XO + C, "maskS": SL, "vm": XO + C, "vso": SL, "sc1": SL, "sc2": SL, "win0": 1376, "win1": 1376, "win2": 1376}),
-    (MX, {"xq": C, "uq": 128, "uq2": 128, "vq": 128, "wq": 512, "wl": 512, "hq": K, "cq": 512,
+    (BF, {"W": 2 * PW + (R + 1) * RX, "ut": 512, "vt": 512, "one": 528, "Z": 528, "rise": C, "cumb": XO + C, "cb": C, "sgn": C,
+          "Bb": 4 * C, "nil": C, "jj": C, "Dg": C, "hc": C, "hp": C, "rs": XO + C, "jnk": C, "big": 32,
+          "E": 4 * K, "H": 4 * K, "tabI": 528, "sdat": C, "segrow": C, "swin": 2 * SL, "ST": 2 * SL, "Dn": SL, "Dp": SL,
+          "maskJ": XO + C, "maskS": XO + SL, "vm": XO + C, "vso": SL, "sc1": SL, "sc2": SL}),
+    (MX, {"xq": C, "uq": 128, "uq2": 256, "vq": 128, "wq": 512, "wl": 512, "hq": K, "cq": 512,
           "eq0": K, "eq1": K, "eq2": K, "lq0": K, "lq1": K, "lq2": K}),
-    (U8, {"xs": C, "us": 128, "us2": 128, "vsc": 128, "wsc": 512, "wls": 512, "hs": K, "cs": 512,
+    (U8, {"xs": C, "us": 128, "us2": 256, "vsc": 128, "wsc": 512, "wls": 512, "hsc": K, "cs": 512,
           "es0": K, "es1": K, "es2": K, "ls0": K, "ls1": K, "ls2": K}),
-    (F32, {"prev": C, "ysb": C, "olb": K, "fc": 8, "col": 16, "cols": 16, "h16": 32, "hh": 16, "lgb": 8, "Cj": 32, "c16": 32,
-           "tabF": 32, "tabM": 32, "tabB": 32, "Fr": C, "junk": C, "acc": 8, "cum": C, "val": C, "T1": C, "seg": C, "sg": 32,
-           "w1": 32, "w2": 32, "ff": 32, "sgn": 32, "vv": 32, "nfb": 32, "FB": 32, "r1": 32, "r2": 32, "r3": 32, "r4": 32, "r5": 32,
+    (F32, {"prev": C, "ysb": C, "olb": K, "cols": 16, "h16": 32, "hh": 16, "c64": 32, "cm": 64,
+           "tabF": 32, "tabM": 32, "tabB": 32, "Fr": C, "acc": 8, "cum": C, "val": C, "T1": C, "seg": C, "sg": 32,
+           "U": C, "jt": C + 16, "pre": 8, "g1": 64, "g2": 64, "fr": 32, "fP": 32, "FB": 32,
+           "r1": 32, "r2": 32, "r3": 32, "r4": 32, "q": 32, "mc": 32, "nf": 32, "own": 32,
            "Bt": 32, "mb": 32, "zs0": 32, "zs1": 32, "zs2": 32, "zl0": 32, "zl1": 32, "zl2": 32}),
-    (I32, {"pint": 8, "ci": 8, "s16": 32, "tgi": 32, "hl": 56, "a0": 32, "a1": 32, "a2": 32, "a3": 32, "a4": 32, "ib": 8, "ob": 8}),
-    (U16, {"eoff": 16, "upo": 8, "LG": 8, "LGk": 2, "rev": 16, "hlu": 56, "spos": 32, "sig": 32, "se": 8, "pos": 32, "voff": 32,
-           "oA": 32, "oB": 32}),
+    (I32, {"pint": 8, "ci": 8, "s16": 32, "tgi": 32, "hl": 56, "a0": 32, "a1": 32, "a2": 32, "a3": 32, "ib": 8, "ob": 8}),
+    (U16, {"eoff": 64, "upo": 16, "J": 8, "Lu": 16, "hlu": 56, "spos": 32, "sig": 32, "se": 8, "oA": 128, "oB": 128}),
 ):
     for _k in _bufs:
         SCRATCH[_k] = ("sbuf", [128, _bufs[_k]], _d)
@@ -33,8 +58,12 @@ SEMAPHORES = (["sv", "sa", "st", "sp", "sent", "dtg", "du", "dx0", "dx1", "dw", 
               + ["rc%d%d" % (_t, _h) for _t in range(R) for _h in range(2)] + ["rl%d" % _t for _t in range(R)])
 
 
+def xo(t):
+    return 2 * PW + RX * t
+
+
 def slot(t):
-    return XO + C + K * (R - 1 - t)
+    return 4 * K * t
 
 
 def rank_program(g, core, T, topo):
@@ -55,8 +84,9 @@ def rank_program(g, core, T, topo):
     log = {}
 
     def V(name, a=0, b=None, step=1):
-        w = SCRATCH[name][1][1]
-        b = w if b is None else b
+        b = SCRATCH[name][1][1] if b is None else b
+        if step < 0:
+            return (T[name][:, b - 1:a - 1:-1], name, a, b, 1)
         view = T[name][:, a:b:step] if step > 1 else T[name][:, a:b]
         if name == "ps":
             return (view, name, a // 512 * 512, (b + 511) // 512 * 512, 1)
@@ -140,9 +170,6 @@ def rank_program(g, core, T, topo):
     def scatter(win, off, in_):
         op("v", lambda: g.vector.tensor_copy(win[0].indirect(off[0]), in_[0]), [off, in_], [win])
 
-    def fill(out, c):
-        op("v", lambda: g.vector.memset(out[0], c), [], [out])
-
     def scan(out, d0, d1, init, op0, op1):
         rd = [d0, d1] + ([] if num(init) else [init])
         op("v", lambda: g.vector.tensor_tensor_scan(out[0], d0[0], d1[0], init if num(init) else init[0], op0, op1), rd, [out])
@@ -150,23 +177,27 @@ def rank_program(g, core, T, topo):
     def turn(out, in_):
         op("v", lambda: g.vector.transpose(out[0], in_[0]), [in_], [out])
 
-    def act(out, in_, func=None, bias=0.0, scale=1.0, acc=None):
-        f = AF.Identity if func is None else func
+    def act(out, in_, func, bias=0.0, scale=1.0, acc=None):
         rd = vs(in_) + [s for s in (bias, scale) if not num(s)]
         b, s = (bias if num(bias) else bias[0]), (scale if num(scale) else scale[0])
         if acc is None:
-            op("a", lambda: g.scalar.activation(out[0], ap(in_), f, bias=b, scale=s), rd, [out])
+            op("a", lambda: g.scalar.activation(out[0], ap(in_), func, bias=b, scale=s), rd, [out])
         else:
-            op("a", lambda: g.scalar.activation(out[0], ap(in_), f, bias=b, scale=s, accum_out=acc[0]), rd, [out, acc])
+            op("a", lambda: g.scalar.activation(out[0], ap(in_), func, bias=b, scale=s, accum_out=acc[0]), rd, [out, acc])
 
-    def afill(out, c):
-        act(out, V("tabI", 0, out[3] - out[2]), scale=0.0, bias=c)
-
-    def times(q, out, in_, c):
+    def lin(q, out, in_, scale=1.0, bias=0.0):
         if q == "a":
-            act(out, in_, scale=c)
+            act(out, in_, AF.Identity, bias, scale)
+        elif num(bias) and scale == 1.0 and bias == 0.0:
+            cp(out, in_)
         else:
-            ts(out, in_, c, A.mult)
+            ts(out, in_, scale, A.mult, bias, A.add)
+
+    def fill(q, out, c):
+        if q == "v":
+            op("v", lambda: g.vector.memset(out[0], c), [], [out])
+        else:
+            act(out, V("one", 0, out[3] - out[2]), AF.Identity, scale=c)
 
     def quant(q, s, in_):
         op("v", lambda: g.vector.quantize_mx(q[0], s[0], in_[0]), [in_], [q, s])
@@ -174,11 +205,11 @@ def rank_program(g, core, T, topo):
     def mm(out, wq, ws, xq, xs):
         op("t", lambda: g.tensor.matmul_mx(out[0], wq[0], ws[0], xq[0], xs[0], True, True), [wq, ws, xq, xs], [out])
 
-    def iota(out, pattern, base, cm, small=True):
-        if small:
-            op("p", lambda: g.iota(out[0], pattern, base, cm, allow_small_or_imprecise_dtypes=True), [], [out])
-        else:
+    def iota(out, pattern, base, cm):
+        if SCRATCH[out[1]][2] == I32:
             op("p", lambda: g.iota(out[0], pattern, base, cm), [], [out])
+        else:
+            op("p", lambda: g.iota(out[0], pattern, base, cm, allow_small_or_imprecise_dtypes=True), [], [out])
 
     def bank(b, w):
         return V("ps", 512 * b, 512 * b + w)
@@ -186,306 +217,250 @@ def rank_program(g, core, T, topo):
     def c1(name, j):
         return V(name, j, j + 1)
 
-    def plane(t, a=0, b=2 * PW):
-        return V("Xh", 2 * PW * t + a, 2 * PW * t + b)
+    def cols(base, a, e, b=None):
+        return V("W", base + 4 * a, base + 4 * e) if b is None else V("W", base + 4 * a + b, base + 4 * e, 4)
 
-    spare = []
+    def state(t):
+        return V("W", xo(t), xo(t) + RX)
 
-    def gap(k=1):
-        for _ in range(k):
-            if spare:
-                spare.pop(0)()
+    def ls28(name):
+        return V(name, 0, 28)
+
+    def diag(name):
+        return V(name, 15, C, 16)
+
+    fi, fs, kc, nthr, k0, r16, init, f4, tiny = [c1("cols", j) for j in range(9)]
+    hi, lo, ends, J = V("hlu", 0, 28), V("hlu", 28, 56), V("se", 2, 4), V("J", 0, 4)
+    halves = [(0, HC), (HC, C)]
+
+    def hb(h, b):
+        return bank((4 + 4 * h + b) % 8, HK)
+
+    def four(name, b):
+        return V(name, 128 * b, 128 * b + 128)
+
+    def firing(S, t, runs):
+        eq, es, zs = "eq%d" % t, "es%d" % t, V("zs%d" % t)
+
+        def run(h, a, e):
+            rb, db, cu, s = bank(2 * h, e - a), bank(2 * h + 1, e - a), V("cumb", XO + a, XO + e), str(h)
+            S["score" + s] = lambda q: [mm(o, four("uq2", j), four("us2", j), V("xq", a, e), V("xs", a, e)) for j, o in enumerate((rb, db))]
+            S["rise" + s] = lambda q: tt(V("rise", a, e), rb, V("prev", a, e), A.is_gt) if t else ts(V("rise", a, e), rb, 0.0, A.is_gt)
+            if t < R - 1:
+                S["prev" + s] = lambda q: lin(q, V("prev", a, e), rb)
+            S["delay" + s] = lambda q: act(V("sgn", a, e), db, AF.Sign, bias=tiny, scale=-1.0)
+            S["count" + s] = lambda q: scan(cu, V("rise", a, e), V("nil", a, e), c1("cumb", XO - 1 + a) if a else -256.0, A.add, A.min)
+            S["steps" + s] = lambda q: lin(q, V("cb", a, e), cu, 32.0, kc)
+            S["reach" + s] = lambda q: act(V("jnk", a, e), cu, AF.Sign, bias=nthr, acc=c1("acc", 2 + h))
+            S["since" + s] = lambda q: scan(V("U", a, e), V("one", a, e), V("cb", a, e), c1("U", a - 1) if a else 0.0, A.add, A.max)
+            S["signed" + s] = lambda q: tt(V("rs", XO + a, XO + e), V("rise", a, e), V("sgn", a, e), A.mult)
+            S["marks" + s] = lambda q: scan(V("vm", XO + a, XO + e, -1), V("cumb", XO - 1 + a, XO - 1 + e, -1), V("rs", XO + a, XO + e, -1),
+                                            0.0, A.min, A.mult)
+
+        def gather(h, b):
+            S["E%d%d" % (h, b)] = lambda q: lin(q, V("E", 4 * HK * h + b, 4 * HK * (h + 1), 4), (state(t), V("eoff", 16 * b + 8 * h, 16 * b + 8 * h + 8)))
+
+        def half(h, a, e):
+            def pack(q):
+                quant(V(eq, a, e), V(es, a, e), V("E", 4 * a, 4 * e))
+                if h:
+                    send(V(es), V("ls%d" % t), "rc%d0" % t)
+                send(V(eq, a, e), V("lq%d" % t, a, e), "rc%d%d" % (t, h), codes=True)
+            S["QE%d" % h] = pack
+            S["vso%d" % h] = lambda q: lin(q, V("vso", 256 * h, 256 * h + 256), (V("vm"), V("sig", 16 * h, 16 * h + 16)), 4.0)
+            for b in range(4):
+                gather(h, b)
+
+        def winners(q):
+            if t:
+                tt(zs, V("r2"), V("Bt"), A.min)
+            else:
+                tt(zs, (V("sc1"), ends), V("r1"), A.add)
+            send(zs, V("zl%d" % t), "rl%d" % t)
+
+        for h, (a, e) in enumerate(runs):
+            run(h, a, e)
+        if len(runs) == 2:
+            S["pre"] = lambda q: lin(q, V("pre", 4, 8), V("pre", 0, 4), 1.0, c1("acc", 2))
+        S["J"] = lambda q: ts(J, V("pre", 4 * len(runs) - 4, 4 * len(runs)), c1("acc", 1 + len(runs)), A.add, -0.5, A.mult)
+        S["g2"] = lambda q: tt(V("g2"), (V("tabI"), J), V("cm"), A.add)
+        S["g1"] = lambda q: tt(V("g1"), (V("U"), J), V("g2"), A.subtract)
+        S["eoff"] = lambda q: ts(V("eoff"), V("g1"), -4.0, A.mult, 4.0 * C, A.min)
+        for h in range(2):
+            half(h, HK * h, HK * (h + 1))
+        S["hc"] = lambda q: scan(V("hc"), V("Dg"), V("cumb", XO, XO + C), -256.0, A.add, A.min)
+        S["hp"] = lambda q: scan(V("hp"), V("Dg"), V("cumb", XO - 1, XO - 1 + C), -256.0, A.add, A.min)
+        S["fr"] = lambda q: tt(ls28("fr"), diag("hc"), diag("hp"), A.subtract)
+        S["nf"] = lambda q: lin(q, ls28("nf"), ls28("fr"), -FAR, FAR)
+        S["fP"] = lambda q: lin(q, ls28("fP"), ls28("fr"), float(PW))
+        S["FB"] = lambda q: tt(ls28("FB"), ls28("nf"), ls28("c64"), A.max)
+        S["sc1"] = lambda q: scan(V("sc1"), V("Dn"), V("vso"), 0.0, A.add, A.min)
+        S["r1"] = lambda q: ts(V("r1"), (V("sc1"), ends), 0.0, A.is_ge, FAR, A.mult)
+        if t:
+            S["r2"] = lambda q: tt(V("r2"), (V("sc1"), ends), V("r1"), A.add)
+        S["zs"] = winners
+        if t == 1:
+            S["Qv"] = lambda q: quant(V("vq"), V("vsc"), V("vt"))
+            S["jt0"] = lambda q: fill(q, V("jt", C, C + 16), -1.0)
+            S["jt1"] = lambda q: lin(q, V("jt", 0, C), V("tabI", 0, C), 1.0, 256.0)
+        if t == R - 1:
+            S["Lu"] = lambda q: ts(V("Lu"), V("g1", 0, 16), -1.0, A.mult, float(C), A.min)
+            S["ol"] = lambda q: (lin(q, V("olb"), (V("jt"), V("Lu"))), dma("s", "dout", T.ol[:], T.olb[0:128:16, :], [V("olb")], []))
+
+    def merging(S, t):
+        lq, ls, zl = "lq%d" % t, "ls%d" % t, ls28("zl%d" % t)
+
+        def element(h, b):
+            a, e = HK * h, HK * (h + 1)
+            out = V("H", 4 * a + b, 4 * e, 4)
+            S["relu%d%d" % (h, b)] = lambda q: act(out, hb(h, b), AF.Relu, scale=0.03125) if q == "a" else ts(out, hb(h, b), 0.0, A.max, 0.03125, A.mult)
+            S["half%d%d" % (h, b)] = lambda q: lin(q, cols(slot(t) + PW, a, e, b), hb(h, b), 0.5)
+            c, d = halves[h]
+            o, B = (28 * b + c // 16, 28 * b + d // 16), V("Bb", 4 * c + b, 4 * d, 4)
+            S["B%d%d" % (h, b)] = lambda q: lin(q, B, (state(t), V("oB", *o)), 0.5)
+            S["add%d%d" % (h, b)] = lambda q: tt(cols(xo(t + 1), c, d, b), (V("W", 0, xo(t) + 4 * C), V("oA", *o)), B, A.add)
+
+        def half(h):
+            a, e = HK * h, HK * (h + 1)
+            c, d = halves[h]
+            S["layer%d" % h] = lambda q: [mm(hb(h, b), four("wl", b), four("wls", b), V(lq, a, e), V(ls, a, e)) for b in range(4)]
+            S["QH%d" % h] = lambda q: (quant(V("hq", a, e), V("hsc", a, e), V("H", 4 * a, 4 * e)),
+                                       [mm(hb(h, b), four("cq", b), four("cs", b), V("hq", a, e), V("hsc", a, e)) for b in range(4)])
+            S["whole%d" % h] = lambda q: lin(q, cols(slot(t), a, e), cols(slot(t) + PW, a, e), 2.0)
+            S["QX%d" % h] = lambda q: quant(V("xq", c, d), V("xs", c, d), cols(xo(t + 1), c, d))
+            for b in range(4):
+                element(h, b)
+            if t == R - 1:
+                S["y%d" % h] = lambda q: (
+                    mm(bank(h, HC), V("vq"), V("vsc"), V("xq", c, d), V("xs", c, d)),
+                    dma("s", "dout", T.oc[:, 4 * c:4 * d], T.xq[:, c:d].bitcast(dt.uint8), [V("xq", c, d)], []),
+                    [dma("sa"[k % 2], "dout", T.osc[4 * k:4 * k + 4, :], T.xs[32 * k:32 * k + 4, :], [V("xs")], []) for k in range(4 * h)])
+                S["ys%d" % h] = lambda q: (lin(q, V("ysb", c, d), bank(h, HC)), dma("a", "dout", T.y[:, c:d], T.ysb[:, c:d], [V("ysb", c, d)], []))
+
+        def places(b):
+            S["oB%d" % b] = lambda q: ts(V("oB", 28 * b, 28 * b + 28), ls28("q"), float(b), A.add, 4.0 * C, A.min)
+            S["oA%d" % b] = lambda q: ts(V("oA", 28 * b, 28 * b + 28), ls28("mc"), float(slot(t + 1) + b), A.add)
+
+        if t < R - 1:
+            S["sc2"] = lambda q: scan(V("sc2"), V("Dp"), V("vso"), 0.0, A.add, A.max)
+            S["r3"] = lambda q: ts(V("r3"), (V("sc2"), ends), 0.0, A.is_le, FAR, A.mult)
+            S["r4"] = lambda q: lin(q, V("r4"), (V("sc2"), ends), -1.0, -4.0 * K)
+            S["Bt"] = lambda q: tt(V("Bt"), V("r4"), V("r3"), A.add)
+        S["own"] = lambda q: lin(q, ls28("own"), ls28("c64"), 1.0, float(xo(t) - slot(t + 1)))
+        S["q"] = lambda q: tt(ls28("q"), zl, ls28("FB"), A.max)
+        S["mb"] = lambda q: tt(ls28("mb"), zl, ls28("fP"), A.add)
+        S["mc"] = lambda q: tt(ls28("mc"), ls28("mb"), ls28("own"), A.min)
+        for k in range(4):
+            places(k)
+        for h in range(2):
+            half(h)
+
+    def starting(S):
+        def counted(name, pattern, base, cm):
+            S["i" + name] = lambda q: iota(V(name), pattern, base, cm)
+
+        def filled(name, out, c):
+            S[name] = lambda q: fill(q, out, c)
+
+        def scaled(name, out, in_, scale, bias=0.0):
+            S[name] = lambda q: lin(q, out, in_, scale, bias)
+
+        def each(k):
+            o = V("upo", 8 * k, 8 * k + 8)
+            S["us%d" % k] = lambda q: op("a", lambda: g.scalar.activation(four("us2", k)[0], T.us[:].indirect(o[0]), AF.Copy), [V("us"), o], [four("us2", k)])
+            S["uq%d" % k] = lambda q: op("v", lambda: g.vector.tensor_copy(four("uq2", k)[0].bitcast(dt.uint32), T.uq[:].bitcast(dt.uint32).indirect(o[0])),
+                                         [V("uq"), o], [four("uq2", k)])
+            scaled("maskS%d" % k, V("maskS", XO + 256 * k, XO + 256 * k + 256), (V("maskJ"), V("sig", 16 * k, 16 * k + 16)), 1.0)
+            S["QX%d" % k] = lambda q: quant(V("xq", *halves[k]), V("xs", *halves[k]), cols(xo(0), *halves[k]))
+
+        def unpacking(b):
+            S["cq%d" % b] = lambda q: quant(four("cq", b), four("cs", b), V("Z", 3 - b, 515 - b))
+
+        for row in (("pint", [[0, 8]], 0, 1), ("hh", [[1, 16]], 0, 0), ("h16", [[16, 32]], 0, 0), ("jj", [[0, 28], [1, 16]], 0, 0),
+                    ("tabI", [[1, 528]], -256, 0), ("cm", [[1, 4], [2048, 16]], 4 * (int(STEP) + 512 + 256), 0),
+                    ("s16", [[0, 16], [16, 2]], 0, 0), ("sdat", [[32, 14], [0, 2], [1, 16]], -255, 0)):
+            counted(*row)
+        for row in (("sw0", V("swin", 0, SL), -256.0), ("sw1", V("swin", SL, 2 * SL), -256.0), ("nil", V("nil"), 0.0), ("tiny", tiny, 2.0 ** -110),
+                    ("pre0", V("pre", 0, 4), 2.0 - C), ("cu0", V("cumb", 0, XO), -256.0), ("vmz", V("vm", 0, XO), 0.0),
+                    ("mj0", V("maskJ", 0, XO), ASIDE), ("ms0", V("maskS", 0, XO), ASIDE), ("big", V("big"), 2.0 ** 20)):
+            filled(*row)
+        for row in (("k0", k0, fi, 2050.0, 32768.0), ("kc", kc, fi, -32.0, STEP + 32 * 263.5), ("nthr", nthr, fi, -16.0, 239.5),
+                    ("f4", f4, fi, 4.0), ("r16", r16, fs, 16.0), ("c64", V("c64"), V("h16"), 4.0, f4),
+                    ("cm", V("cm"), V("cm"), 0.25), ("sdat", V("sdat"), V("sdat"), 1.0, r16),
+                    ("tF1", V("tabF", 16, 32), V("tabF", 0, 16), 1024.0), ("tM0", V("tabM", 0, 16), V("tabF", 0, 16), 1.0),
+                    ("tM1", V("tabM", 16, 32), V("tabF", 0, 16), 2.0 ** -10), ("init", init, c1("acc", 0), 1.0, k0),
+                    ("Fr", V("Fr"), (V("tabF"), hi), 1.0), ("maskJ", V("maskJ", XO, XO + C), (V("tabF", 0, 16), lo), ASIDE),
+                    ("Dp", V("Dp"), V("Dn"), -1.0)):
+            scaled(*row)
+        for k in range(2):
+            each(k)
+        for b in range(4):
+            unpacking(b)
+        S["one"] = lambda q: fill("v", V("one"), 1.0)
+        S["pad"] = lambda q: fill("v", V("W", xo(0) + 4 * C, xo(R), RX), 0.0)
+        S["Z"] = lambda q: op("p", lambda: g.affine_select(T.Z[:], T.one[:], [[-1, 528]], A.is_equal, 0.0, 3, 4), [V("one")], [V("Z")])
+        S["ci0"] = lambda q: ts(c1("ci", 0), c1("pint", 0), 15, A.bitwise_and)
+        S["ci1"] = lambda q: ts(c1("ci", 1), c1("pint", 0), 4, A.arith_shift_right, 1, A.bitwise_and)
+        S["fi"] = lambda q: cp(V("cols", 0, 2), V("ci", 0, 2))
+        S["tB0"] = lambda q: ts(V("tabB", 0, 16), V("hh"), fi, A.is_lt, 1024.0, A.add)
+        S["tB1"] = lambda q: ts(V("tabB", 16, 32), V("hh"), fi, A.is_lt, 1024.0, A.mult)
+        S["tF0"] = lambda q: ts(V("tabF", 0, 16), V("hh"), fi, A.is_equal)
+        S["up0"] = lambda q: cp(V("upo", 0, 8), V("h16", 0, 8))
+        S["up1"] = lambda q: ts(V("upo", 8, 16), V("h16", 0, 8), 1.0, A.add)
+        S["segrow"] = lambda q: act(V("segrow"), V("jj"), AF.Sign)
+        S["Dg"] = lambda q: ts(V("Dg"), V("jj"), fi, A.is_equal, 1024.0, A.mult)
+        S["Qu"] = lambda q: quant(V("uq"), V("us"), V("ut"))
+        S["sendW"] = lambda q: (send(V("wq"), V("wl"), "rw", codes=True), send(V("wsc"), V("wls"), "rw"))
+        S["hi"] = lambda q: ts(V("hl", 0, 28), ls28("tgi"), 4, A.arith_shift_right)
+        S["lo"] = lambda q: ts(V("hl", 28, 56), ls28("tgi"), 15, A.bitwise_and)
+        S["hlu"] = lambda q: cp(V("hlu"), V("hl"))
+        S["acc"] = lambda q: act(V("seg"), (V("tabB"), hi), AF.Identity, acc=c1("acc", 0))
+        S["cum"] = lambda q: scan(V("cum"), V("Fr"), V("Fr"), init, A.add, A.max)
+        S["val"] = lambda q: tt(V("val"), (V("tabM"), hi), V("cum"), A.mult)
+        S["T1"] = lambda q: turn(V("T1"), V("val"))
+        S["seg"] = lambda q: scan(V("seg"), V("segrow"), V("T1"), 0.0, A.mult, A.add)
+        S["a0"] = lambda q: cp(ls28("a0"), diag("seg"))
+        S["a1"] = lambda q: ts(ls28("a1"), ls28("a0"), 1023, A.bitwise_and)
+        S["a2"] = lambda q: ts(ls28("a2"), ls28("a0"), 1008, A.bitwise_and)
+        S["a3"] = lambda q: tt(ls28("a3"), ls28("a1"), ls28("s16"), A.add)
+        S["a4"] = lambda q: tt(ls28("a0"), ls28("a3"), ls28("a2"), A.add)
+        S["spos"] = lambda q: cp(ls28("spos"), ls28("a0"))
+        S["ib0"] = lambda q: cp(c1("ib", 0), init)
+        S["ib1"] = lambda q: ts(c1("ib", 1), c1("cum", C - 1), 1025.0, A.add)
+        S["ob0"] = lambda q: ts(V("ob", 0, 4, 2), V("ib", 0, 2), 1023, A.bitwise_and)
+        S["ob1"] = lambda q: ts(V("ob", 1, 4, 2), V("ib", 0, 2), 10, A.arith_shift_right)
+        S["se"] = lambda q: cp(V("se", 0, 4), V("ob", 0, 4))
+        S["scatter"] = lambda q: scatter(V("swin"), ls28("spos"), V("sdat"))
+        S["ST"] = lambda q: turn(V("ST"), V("swin"))
+        S["sg"] = lambda q: tt(V("sg"), V("ST", 0, 2 * SL, 32), V("ST", 16, 2 * SL, 32), A.add)
+        S["sig"] = lambda q: ts(V("sig"), V("sg"), 512.0 + XO - 1, A.add)
+        S["Dn"] = lambda q: tt(V("Dn"), (V("maskJ"), V("sig")), V("maskS", XO - 1, XO + SL - 1), A.subtract)
+        S["open"] = lambda q: scatter(V("Dn"), V("se", 0, 2), V("big"))
 
     dma("s", "dtg", T.tgi[:, 0:28], T.tg[:], [], [V("tgi")])
     dma("a", "du", T.ut[:], T.u[:], [], [V("ut")])
-    for h in range(2):
-        dma("s", "dx%d" % h, T.X[:, 4 * HC * h:4 * HC * (h + 1)], T.x[:, 4 * HC * h:4 * HC * (h + 1)], [], [V("X", 4 * HC * h, 4 * HC * (h + 1))])
+    for h, (a, e) in enumerate(halves):
+        dma("s", "dx%d" % h, cols(xo(0), a, e)[0], T.x[:, 4 * a:4 * e], [], [cols(xo(0), a, e)])
     dma("s", "dw", T.wq[:].bitcast(dt.uint8), T.wc[:], [], [V("wq")])
     dma("s", "dw", T.wsc[:], T.ws[:], [], [V("wsc")])
     dma("s", "dv", T.vt[:], T.v[:], [], [V("vt")])
-
-    iota(c1("pint", 0), [[0, 1]], 0, 1, small=False)
-    iota(c1("pint", 1), [[0, 1]], 0, 17, small=False)
-    iota(V("hh"), [[1, 16]], 0, 0)
-    iota(V("h16"), [[16, 32]], 0, 0)
-    iota(V("lgb", 0, 6), [[1, 3], [256, 2]], 0, 0)
-    iota(V("tabI"), [[1, 528]], -256, 0)
-    iota(V("sd0"), [[32, 14], [0, 2], [1, 16]], -255, 0)
-    iota(V("s16", 0, 28), [[0, 14], [16, 2]], 0, 0, small=False)
-    fill(V("one"), 1.0)
-    op("p", lambda: g.affine_select(T.Z[:], T.one[:], [[-1, 528]], A.is_equal, 0.0, 3, 4), [V("one")], [V("Z")])
-    ts(c1("ci", 0), c1("pint", 0), 15, A.bitwise_and)
-    ts(V("ci", 1, 3), V("pint", 0, 2), 4, A.arith_shift_right, 1, A.bitwise_and)
-    fill(V("Rw"), 0.0)
-    cp(V("fc", 0, 3), V("ci", 0, 3))
-    fill(V("win0", KO - 16, 1376), -256.0)
-    fi, fs, fx = c1("fc", 0), c1("fc", 1), c1("fc", 2)
-    initc, pm = c1("col", 0), c1("col", 1)
-    d0c, i16, y, y2, k0, r16, init, f16 = [c1("cols", j) for j in range(8)]
-    ts(V("tabB", 0, 16), V("hh"), fi, A.is_lt, 1024.0, A.add)
-    ts(V("tabB", 16, 32), V("hh"), fi, A.is_lt, 1024.0, A.mult)
-    ts(V("tabF", 0, 16), V("hh"), fi, A.is_equal)
-    ts(V("tabF", 16, 32), V("hh"), fi, A.is_equal, 1024.0, A.mult)
-    ts(pm, fi, 2.0, A.not_equal)
-    ts(initc, fi, 0.0, A.is_equal, 256.0, A.mult)
-    ts(k0, fi, 1025.0, A.mult, 16384.0, A.add)
-    ts(f16, fi, float(XO), A.add)
-    act(i16, fi, scale=16.0)
-    act(r16, fs, scale=16.0)
-    act(y, fx, scale=464.0, bias=i16)
-    act(y2, fx, scale=272.0, bias=i16)
-    act(V("c16"), V("h16"), bias=f16)
-    act(V("tabM", 0, 16), V("tabF", 0, 16))
-    act(V("tabM", 16, 32), V("tabF", 0, 16), scale=2.0 ** -10)
-    ts(V("upo"), V("h16", 0, 8), pm, A.subtract, 1.0, A.add)
-    ts(d0c, initc, -4.0, A.mult, 1.0, A.add)
-    ts(V("Cj"), V("h16"), fi, A.add, float(C), A.add)
-    fill(V("Xh", XO - 1, 8 * PW, 2 * PW), 0.0)
-    fill(V("TT", 928, 976), 0.0)
-    fill(V("vm", 0, XO), 0.0)
-    fill(V("maskJ", 0, XO), 0.0)
-    ts(V("LG", 0, 6), V("lgb", 0, 6), y, A.add)
-    cp(c1("LGk", 0), y2)
-
-    hi, lo = V("hlu", 0, 28), V("hlu", 28, 56)
-    ts(V("hl", 0, 28), V("tgi", 0, 28), 4, A.arith_shift_right)
-    ts(V("hl", 28, 56), V("tgi", 0, 28), 15, A.bitwise_and)
-    quant(V("uq"), V("us"), V("ut"))
-    cp(V("hlu"), V("hl"))
-    op("a", lambda: g.scalar.activation(T.us2[:], T.us[:].indirect(T.upo[:]), AF.Copy), [V("us"), V("upo")], [V("us2")])
-    act(V("junk"), (V("tabB"), hi), acc=c1("acc", 0))
-    act(init, c1("acc", 0), bias=k0)
-    act(V("d0"), V("tabI", 0, C), scale=0.0, bias=d0c)
-    afill(V("segrow"), 1.0)
-    act(V("segrow", 0, C, 16), V("h16", 0, 28), scale=0.0)
-    act(V("sdat"), V("sd0"), bias=r16)
-    afill(V("swin", 0, SL), -256.0)
-    afill(V("swin", SL, 2 * SL), -256.0)
-    op("v", lambda: g.vector.tensor_copy(T.uq2[:].bitcast(dt.uint32), T.uq[:].bitcast(dt.uint32).indirect(T.upo[:])), [V("uq"), V("upo")], [V("uq2")])
-    cp(V("Fr"), (V("tabF"), hi))
-
-    sort_calls = [
-        lambda: scan(V("cum"), V("Fr"), V("Fr"), init, A.add, A.max),
-        lambda: tt(V("val"), (V("tabM"), hi), V("cum"), A.mult),
-        lambda: turn(V("T1"), V("val")),
-        lambda: scan(V("seg"), V("segrow"), V("T1"), 0.0, A.mult, A.add),
-        lambda: cp(V("a0", 0, 28), V("seg", 15, C, 16)),
-        lambda: (ts(V("a1", 0, 28), V("a0", 0, 28), 1023, A.bitwise_and), ts(V("a2", 0, 28), V("a0", 0, 28), 1008, A.bitwise_and)),
-        lambda: tt(V("a3", 0, 28), V("a1", 0, 28), V("s16", 0, 28), A.add),
-        lambda: tt(V("a4", 0, 28), V("a3", 0, 28), V("a2", 0, 28), A.add),
-        lambda: cp(V("spos", 0, 28), V("a4", 0, 28)),
-    ]
-
-    def sort_scatter():
-        cp(c1("ib", 0), init)
-        cp(c1("ib", 1), c1("cum", C - 1))
-        fill(V("zer"), 0.0)
-        scatter(V("swin"), V("spos", 0, 28), V("sdat"))
-        ts(V("ob", 0, 4, 2), V("ib", 0, 2), 1023, A.bitwise_and)
-        ts(V("ob", 1, 4, 2), V("ib", 0, 2), 10, A.arith_shift_right)
-
-    def sort_order():
-        turn(V("ST"), V("swin"))
-        cp(V("se", 0, 4), V("ob", 0, 4))
-        tt(V("sg", 0, 30), V("ST", 0, 2 * SL, 32), V("ST", 16, 2 * SL, 32), A.add)
-        scatter(V("cont"), V("se", 0, 2), V("zer"))
-        ts(V("sig", 0, 30), V("sg", 0, 30), 512.0 + XO - 1, A.add)
-        act(V("maskS"), (V("maskJ"), V("sig", 0, 30)))
-
-    def score(h, sq, ss):
-        a, b = HC * h, HC * (h + 1)
-        q, s = V("xq", a, b), V("xs", a, b)
-        quant(q, s, V("X", 4 * a, 4 * b))
-        mm(bank(h, HC), V(sq), V(ss), q, s)
-
-    def rises(t, h):
-        a, e = HC * h, HC * (h + 1)
-        if t == 0:
-            ts(V("rise", a, e), bank(h, HC), 0.0, A.is_gt)
-        else:
-            tt(V("rise", a, e), bank(h, HC), V("prev", a, e), A.is_gt)
-        if t < R - 1:
-            act(V("prev", a, e), bank(h, HC), scale=pm)
-
-    def count(h):
-        a, e = HC * h, HC * (h + 1)
-        scan(V("Rw", 16 + a, 16 + e), V("d0", a, e), V("rise", a, e), initc if h == 0 else c1("Rw", 15 + a), A.max, A.subtract)
-
-    def turn_a(h):
-        turn(V("TT", HC * h, HC * (h + 1)), V("Rw", 16 + HC * h, 16 + HC * (h + 1)))
-
-    def turn_b(h):
-        turn(V("TT", C + HC * h, C + HC * (h + 1) + 32 * h), V("Rw", HC * h, HC * (h + 1) + 32 * h))
-
-    def second(t):
-        rises(t, 0)
-        score(1, "uq2", "us2")
-        count(0)
-        gap()
-        turn_a(0)
-
-    def kept(h):
-        for b in range(4):
-            act(V("Bb", C * b + HC * h, C * b + HC * (h + 1)), (plane(b, 0, XO + C), V("oB", 14 * h, 14 * h + 14)))
-
-    def merge(t, last):
-        lq, ls, zl = "lq%d" % t, "ls%d" % t, "zl%d" % t
-        landed("rl%d" % t, ne, [V(zl)])
-        landed("rc%d0" % t, 2 * ne, [V(lq, 0, HK), V(ls)])
-        landed("rc%d1" % t, ne, [V(lq, HK, K)])
-        db = [[bank((2 + 4 * h + b) % 8, HK) for b in range(4)] for h in range(2)]
-        for h in range(2):
-            a, e = HK * h, HK * (h + 1)
-            for b in range(4):
-                mm(db[h][b], V("wl", 128 * b, 128 * b + 128), V("wls", 128 * b, 128 * b + 128), V(lq, a, e), V(ls, a, e))
-        for h in range(2):
-            a, e = HK * h, HK * (h + 1)
-            for b in range(0, 4, 2):
-                ts(V("H", 4 * a + b, 4 * e, 4), db[h][b], 0.0, A.max, 0.03125, A.mult)
-                act(V("H", 4 * a + b + 1, 4 * e, 4), db[h][b + 1], func=AF.Relu, scale=0.03125)
-            quant(V("hq", a, e), V("hs", a, e), V("H", 4 * a, 4 * e))
-            for b in range(4):
-                mm(db[h][b], V("cq", 128 * b, 128 * b + 128), V("cs", 128 * b, 128 * b + 128), V("hq", a, e), V("hs", a, e))
-
-        def half(h, b, q):
-            times(q, plane(b, slot(t) + HK * h, slot(t) + HK * (h + 1)), db[h][b], 0.5)
-
-        def whole(h, b, q):
-            a, e = slot(t) + HK * h, slot(t) + HK * (h + 1)
-            times(q, plane(b, PW + a, PW + e), plane(b, a, e), 2.0)
-
-        def add(h, b):
-            a, e = HC * h, HC * (h + 1)
-            tt(V("X", 4 * a + b, 4 * e, 4), (plane(b), V("oA", 14 * h, 14 * h + 14)), V("Bb", C * b + a, C * b + e), A.add)
-
-        for b in range(4):
-            half(0, b, "a")
-        tt(V("mb"), V(zl), V("nfb"), A.add)
-        whole(0, 0, "v")
-        cp(V("oA"), V("mb"))
-        whole(0, 1, "v")
-        for b in range(4):
-            half(1, b, "va"[b % 2])
-        whole(0, 2, "v")
-        whole(1, 0, "v")
-        whole(0, 3, "a")
-        for b in range(1, 4):
-            whole(1, b, "a")
-        kept(1)
-        for b in range(4):
-            add(0, b)
-        add(1, 0)
-        score(0, "vq" if last else "uq2", "vsc" if last else "us2")
-        if last:
-            store(0)
-        for b in range(1, 4):
-            add(1, b)
-        if last:
-            score(1, "vq", "vsc")
-            store(1)
-        else:
-            second(t + 1)
-
-    def store(h):
-        a, e = HC * h, HC * (h + 1)
-        dma("s", "dout", T.oc[:, 4 * a:4 * e], T.xq[:, a:e].bitcast(dt.uint8), [V("xq", a, e)], [])
-        if h == 1:
-            for k in range(4):
-                dma("sa"[k % 2], "dout", T.osc[4 * k:4 * k + 4, :], T.xs[32 * k:32 * k + 4, :], [V("xs")], [])
-        act(V("ysb", a, e), bank(h, HC))
-        dma("a", "dout", T.y[:, a:e], T.ysb[:, a:e], [V("ysb", a, e)], [])
-
-    def fire(t):
-        win, eq, es, lq = "win%d" % t, "eq%d" % t, "es%d" % t, "lq%d" % t
-        for b in range(4):
-            act(plane(b, XO, XO + C), V("X", b, 4 * C, 4), scale=0.5)
-        rises(t, 1)
-        turn_b(0)
-        count(1)
-        gap()
-        turn_a(1)
-        turn_b(1)
-        if t == 0:
-            act(V("maskJ", XO, XO + C), (V("tabF", 0, 16), lo))
-            afill(V("cont"), 1.0)
-        else:
-            for b in range(4):
-                act(plane(b, PW + XO, PW + XO + C), V("X", b, 4 * C, 4))
-        gap()
-        tt(V("w1"), (V("TT"), V("LG", 2, 4)), V("Cj"), A.mult)
-        ts(V("sgn"), (V("TT"), V("LG", 4, 6)), 2.0, A.mult, -1.0, A.add)
-        tt(V("w2"), (V("TT"), V("LG", 0, 2)), V("w1"), A.subtract)
-        gap()
-        ts(V("pos"), V("w2"), float(KO), A.add)
-        ts(V("ff"), V("w2"), 1.0, A.add, 0.0, A.max)
-        gap()
-        scatter(V(win), V("pos", 0, 28), V("tabI", 1, 1 + C))
-        tt(V("vv"), V("ff"), V("sgn"), A.mult)
-        turn(V("TK", 0, K), V(win, KO, KO + K))
-        turn(V("TK", K, K + 288), V(win, KO - 16, 1376))
-        ts(V("voff"), V("vv"), 256.0, A.add)
-        ts(V("eoff"), (V("TK"), c1("LGk", 0)), 255.0 + XO, A.add)
-        ts(V("nfb"), V("w2"), -0.5, A.is_lt, float(PW), A.mult)
-        for h in range(2):
-            a, e = HK * h, HK * (h + 1)
-            for b in range(4):
-                times("a" if t == 0 or b % 2 else "v", V("E", 4 * a + b, 4 * e, 4), (plane(b, 0, XO + C), V("eoff", 8 * h, 8 * h + 8)), 2.0)
-            if t == 0 and h == 0:
-                gap(len(spare))
-                sort_scatter()
-            quant(V(eq, a, e), V(es, a, e), V("E", 4 * a, 4 * e))
-            if h == 1:
-                send(V(es), V("ls%d" % t), "rc%d0" % t)
-            send(V(eq, a, e), V(lq, a, e), "rc%d%d" % (t, h), codes=True)
-        act(V("vm", XO, XO + C), (V("tabI"), V("voff", 0, 28)))
-
-    def route(t):
-        ends = V("se", 2, 4)
-        tt(V("FB"), V("c16"), V("nfb"), A.subtract)
-        if t < R - 1:
-            fill(V("win%d" % (t + 1), KO - 16, 1376), -256.0)
-        ts(V("oB"), V("FB"), XO - 1.0, A.max)
-        tt(V("vso"), (V("vm"), V("sig", 0, 30)), V("maskS"), A.mult)
-        kept(0)
-        scan(V("sc1"), V("cont"), V("vso"), 0.0, A.mult, A.max)
-        ts(V("r1"), (V("sc1"), ends), 0.0, A.is_gt, float(slot(t) - 1), A.mult)
-        tt(V("r2"), (V("sc1"), ends), V("r1"), A.add)
-        tt(V("zs%d" % t), V("r2"), V("c16" if t == 0 else "Bt"), A.max)
-        send(V("zs%d" % t), V("zl%d" % t), "rl%d" % t)
-        if t == 0:
-            for b in range(4):
-                ts(plane(b, PW + XO, PW + XO + C), plane(b, XO, XO + C), 2.0, A.mult)
-        if t < R - 1:
-            scan(V("sc2"), V("cont"), V("vso"), 0.0, A.mult, A.min)
-            spare.extend([
-                lambda: ts(V("r3"), (V("sc2"), ends), 0.0, A.is_lt, float(1 - slot(t)), A.mult),
-                lambda: tt(V("r4"), (V("sc2"), ends), V("r3"), A.add),
-                lambda: ts(V("r5"), V("r4"), -1.0, A.mult),
-                lambda: tt(V("Bt"), V("r5"), V("c16"), A.max),
-            ])
-
-    send(V("wq"), V("wl"), "rw", codes=True)
-    send(V("wsc"), V("wls"), "rw")
     landed("rw", 2 * ne, [V("wl"), V("wls")])
-    spare.extend(sort_calls)
-    score(0, "uq2", "us2")
-    gap(2)
-    second(0)
     for t in range(R):
-        fire(t)
-        if t == 0:
-            sort_order()
-            for b in range(4):
-                quant(V("cq", 128 * b, 128 * b + 128), V("cs", 128 * b, 128 * b + 128), V("Z", 3 - b, 515 - b))
-        gap(len(spare))
-        route(t)
-        if t == 1:
-            ts(V("rev"), V("c16", 0, 16), -1.0, A.mult, 255.0 + XO, A.add)
-            quant(V("vq"), V("vsc"), V("vt"))
-        if t == R - 1:
-            act(V("olb"), (V("win%d" % t, KO, KO + K), V("rev")), bias=255.0)
-            dma("s", "dout", T.ol[:], T.olb[0:128:16, :], [V("olb")], [])
-        merge(t, t == R - 1)
+        landed("rl%d" % t, ne, [V("zl%d" % t)])
+        landed("rc%d0" % t, 2 * ne, [V("lq%d" % t, 0, HK), V("ls%d" % t)])
+        landed("rc%d1" % t, ne, [V("lq%d" % t, HK, K)])
+
+    steps = [{} for _ in range(R + 1)]
+    starting(steps[0])
+    for t in range(R):
+        firing(steps[t], t, halves if t else [(0, C)])
+        merging(steps[t + 1], t)
+    for t, order in enumerate([START] + [ROUND] * (R - 1) + [END]):
+        for word in order.split():
+            name, q = (word + ":v").split(":")[:2]
+            S = steps[t + {"+": 1, "-": -1}.get(name[0], 0)]
+            if name.strip("+-") in S:
+                S.pop(name.strip("+-"))(q)
 
     for sem in cnt:
         wait("p", sem, cnt[sem], {})

@@ -3,7 +3,9 @@ from concourse.mybir import dt, AluOpType, ActivationFunctionType
 C, K, R = 448, 256, 3
 HC = C // 2
 HK = K // 2
+RUNS = [(0, 256), (256, C)]
 XO = 16
+ZO = 16
 RX = 4 * C + 16
 PW = R * 4 * K
 FAR = 32768.0
@@ -13,49 +15,52 @@ SL = 512
 F32, BF, I32, U16, U8, MX = "float32", "bfloat16", "int32", "uint16", "uint8", "float8_e4m3fn_x4"
 
 START = """
-    ih16 ihh one up0 pad mj0:v up1 ipint ci1 ci0 ms0:a fi tF0 vmz:v nil:a cu0:a icm tB0 tM1:a ijj tB1 tM0:a pre0:a tF1:v
-    lo Z cm:a hi hlu is16 acc k0:v Fr:a tiny:v isdat Qu Dg init:a us0 itabI sw0:a uq0 us1 uq1 +jt0:a kc:a nthr:a
-    QX0 cq0 segrow r16:a cum QX1 sw1:a sendW score0 val f4:a ib1 rise0 ib0 count0 T1 ob0 reach0 seg steps0:a
-    J a0 g2 sdat:a since0 a2 a1 g1 a3 big:a eoff delay0 a4 E01:a ob1 spos E02:a hc E13:a E00:a E03:a E10:a E11:a
-    scatter E12:a ST QE0 sg QE1 sig maskJ:a signed0 maskS1:a se marks0 maskS0:a Dn cq3 vso1:a +layer0 vso0:a open
-    prev0:a cq2 sc1 +relu01:a +relu02:a c64:v +layer1 +relu03:a r1 zs +relu00:v +relu11:a +relu12:a cq1 +QH0 hp
-    +relu13:a +own:v +relu10:a fr +QH1 fP:v Dp:a +Qv +half01:a +sc2 nf:a FB +half02:v +r3 +q +mb +oB0 +half10:a
-    +half00:a +mc +half03:a +oB1 +r4:v +half12:a +half13:a +oB3 +half11:a +oB2 +whole0:a +whole1:v
-    +oA1 +B01:a +oA2 +oA3 +B00:a +Bt +oA0"""
+    one nil:v pre0:a ipint cu0:v ih16 ci1 ci0 ihh fi pad k0:v tB1 up0 tF0 hi tk0:v lo sw1:a cu1:a tF1:v ijj icm tB0 is16
+    fib:a hlu Qu tM1:v tM0:a acc up1 Hm uq1 QX0 uq0 Z us0 isdat Fr:a cq0 mj0:v r16:a tgu ip17 us1 cm:a i16:a nthr:a
+    init:v QX1 f4:a kc:a score0 itabI c64:a cum segrow hf:a ib0 rise0 prev0:a val count0 T1 sw0:a ms0:a ci2 reach0
+    steps0:a tiny:v seg J fx a0 sdat:a vmz:a since0 a1 g2 delay0 maskJ:a ib1 a2 a3 g1 a4 LG sendW eoff
+    E02:a E03:a spos cq1 scatter E01:a Lu E00:a E13:a ob0 E12:a QE0 E11:a ST ob1 sg E10:a tr0:a QE1 sig +own:a trow:a
+    maskS0:a marks0 vso0:a maskS1:v se Dn +jt0:a big:a cq3 open vso1:a sc1 cq2 +tk:a r1 idle Dp:a +Qv zs
+    +tu1 +layer0 +tu0 held +oN3 +relu00:a +oN1 +relu01:a +relu02:a +layer1 +sc2 +relu03:a +QH0 +Xn03:a +relu10:a +oN2
+    +relu13:a +oN0 +relu12:a +relu11:v +Xn01:v +Xn11:a +whole02:a +r3 +Xn12:a +QH1 +Xn02:v +whole00:v fP +mean02
+    +Xn10:a +mean01 +mean10 +mean03 +Xn00:a +whole13:v +mean12 +Xn13:a +mean11 +whole10:a +mb +mean00 +whole01:a +mc
+    +r4:a +whole12:a +mean13 +oA1 +whole03:a +oA3 +oA0 +Bt +whole11:a +oA2"""
 ROUND = """
-    add01 B03:a add00 B02:a add03 B10:a B11:a add02 add10 B12:a QX0 add11 score0 add12 rise0 B13:a add13
-    count0 delay0 +own:a prev0:a QX1 score1 signed0 steps0:a rise1 reach0 delay1 since0 pre:a count1 signed1 marks0
-    reach1 steps1:a marks1 J since1 vso1:a vso0:a g2 g1 eoff
-    sc1 E02:a r1 r2 E00:a E01:v zs E03:a E11:a QE0 E10:a E12:a E13:v QE1
-    hc hp fr fP:v nf:v jt1:a +sc2 FB +layer0 +mb +q prev1:a +r4:a +oB1 +oB0 +B01:a +oB2
-    +relu01:a +mc +r3 +relu02:a +B00:v +layer1 +relu10:a +relu00:v +relu03:v +Bt +QH0 +oA1 +relu12:a +relu11:v +relu13:a +oA0 +QH1
-    +half00:a +half01:a +half03:a +half02:v +oB3 +half10:a +oA2 +half11:a +whole0:v +half12:a +half13:v +oA3 +whole1:v"""
+    X01:a X00:v X02:a X10:a X13:a X03:v QX0 score0 X11:a delay0 X12:v rise0 QX1 count0 score1 rise1 count1 prev0:a
+    marks0 reach0 steps0:a pre:a delay1 since0 reach1 marks1 +own:v J steps1:a since1 +Xo0:a vso0:a g2 vso1:a g1 eoff Lu
+    E02:a E03:a E12:a +again E11:v E01:v E00:v E10:a E13:v QE0 sc1 QE1
+    +Xo1:a r1 +Xo3:v r2 idle +meano0 zs +Xo2:a held +tk:a +meano1 +meano3 +tu1 jt1:a +tu0 +meano2 +oN2 fP +oN0
+    +layer0 prev1:a +layer1 +Xn02:a +oN1 +sc2 +oN3 +Xn12:v +Xn01:a +Xn00:a +Xn03:v +Xn13:a
+    +relu00:v +relu01:a +relu02:v +relu03:v +mb +relu10:a +QH0 +relu11:a +relu13:v +r3 +relu12:a +r4:a +mc +QH1
+    +mean00 +whole02:v +Xn11:a +mean03 +Xn10:a +oA1 +whole00:a +whole10:a +mean11 +whole12:a +mean01 +mean02 +mean10
+    +mean12 +whole13:a +mean13 +whole03:a +oA0 +whole01:a +whole11:a +oA2 +Bt +oA3"""
 END = """
-    -Lu B03:a B02:a add00 B10:a add01 -ol:a add03 add02 add10 B11:a QX0 B12:a y0 add11 B13:a ys0:a add12 add13 QX1 y1 ys1:v"""
+    X01:a X00:v X03:a X02:v QX0 y0 X13:a X10:v X11:a X12:v QX1 ys0:a y1 -ol:v ys1:a"""
 
 SCRATCH = {"ps": ("psum", [128, 4096], F32)}
 for _d, _bufs in (
-    (BF, {"W": 2 * PW + (R + 1) * RX, "ut": 512, "vt": 512, "one": 528, "Z": 528, "rise": C, "cumb": XO + C, "cb": C, "sgn": C,
-          "Bb": 4 * C, "nil": C, "jj": C, "Dg": C, "hc": C, "hp": C, "rs": XO + C, "jnk": C, "big": 32,
+    (BF, {"W": 2 * PW + (R + 1) * RX, "ut": 512, "vt": 512, "one": 528, "Z": 528, "cz": 2 * (ZO + C), "rz": 2 * (ZO + C), "cb": C,
+          "Xn": 4 * K, "Xo": 4 * K, "trow": C + 16, "tk": K + 32, "TK": 2 * K + 32, "nil": 528, "jj": C, "Hm": C, "hc": C, "hp": C, "jnk": C, "big": 32, "fib": 16,
           "E": 4 * K, "H": 4 * K, "tabI": 528, "sdat": C, "segrow": C, "swin": 2 * SL, "ST": 2 * SL, "Dn": SL, "Dp": SL,
-          "maskJ": XO + C, "maskS": XO + SL, "vm": XO + C, "vso": SL, "sc1": SL, "sc2": SL}),
-    (MX, {"xq": C, "uq": 128, "uq2": 256, "vq": 128, "wq": 512, "wl": 512, "hq": K, "cq": 512,
+          "maskJ": 2 * (ZO + C), "maskS": XO + SL, "vm": 2 * (ZO + C), "vso": SL, "sc1": SL, "sc2": SL}),
+    (MX, {"xq": C, "uq": 128, "uq2": 256, "vq": 128, "wq": 512, "wl": 512, "hq": R * K, "cq": 512,
           "eq0": K, "eq1": K, "eq2": K, "lq0": K, "lq1": K, "lq2": K}),
-    (U8, {"xs": C, "us": 128, "us2": 256, "vsc": 128, "wsc": 512, "wls": 512, "hsc": K, "cs": 512,
+    (U8, {"xs": C, "us": 128, "us2": 256, "vsc": 128, "wsc": 512, "wls": 512, "hsc": R * K, "cs": 512,
           "es0": K, "es1": K, "es2": K, "ls0": K, "ls1": K, "ls2": K}),
     (F32, {"prev": C, "ysb": C, "olb": K, "cols": 16, "h16": 32, "hh": 16, "c64": 32, "cm": 64,
            "tabF": 32, "tabM": 32, "tabB": 32, "Fr": C, "acc": 8, "cum": C, "val": C, "T1": C, "seg": C, "sg": 32,
-           "U": C, "jt": C + 16, "pre": 8, "g1": 64, "g2": 64, "fr": 32, "fP": 32, "FB": 32,
-           "r1": 32, "r2": 32, "r3": 32, "r4": 32, "q": 32, "mc": 32, "nf": 32, "own": 32,
+           "U": C, "jt": C + 16, "pre": 8, "g1": 64, "g2": 64, "fP": 32,
+           "r1": 32, "r2": 32, "r3": 32, "r4": 32, "mc": 32, "own": 32,
            "Bt": 32, "mb": 32, "zs0": 32, "zs1": 32, "zs2": 32, "zl0": 32, "zl1": 32, "zl2": 32}),
     (I32, {"pint": 8, "ci": 8, "s16": 32, "tgi": 32, "hl": 56, "a0": 32, "a1": 32, "a2": 32, "a3": 32, "ib": 8, "ob": 8}),
-    (U16, {"eoff": 64, "upo": 16, "J": 8, "Lu": 16, "hlu": 56, "spos": 32, "sig": 32, "se": 8, "oA": 128, "oB": 128}),
+    (U16, {"eoff": 64, "upo": 16, "J": 8, "Lu": 16 * R, "Ll": 16 * R, "tgu": 32, "tgl": 32, "LG": 2, "oN": 64 * R,
+           "hlu": 56, "spos": 32, "sig": 32, "se": 8, "oA": 128}),
 ):
     for _k in _bufs:
         SCRATCH[_k] = ("sbuf", [128, _bufs[_k]], _d)
 
-SEMAPHORES = (["sv", "sa", "st", "sp", "sent", "dtg", "du", "dx0", "dx1", "dw", "dv", "dout", "rw"]
-              + ["rc%d%d" % (_t, _h) for _t in range(R) for _h in range(2)] + ["rl%d" % _t for _t in range(R)])
+SEMAPHORES = (["sv", "sa", "st", "sp", "sent", "dtg", "du", "dx0", "dx1", "dw", "dv", "dout", "rw", "rt"]
+              + ["rc%d%d" % (_t, _h) for _t in range(R) for _h in range(2)] + ["r%s%d" % (_k, _t) for _k in "le" for _t in range(R)])
 
 
 def xo(t):
@@ -197,7 +202,7 @@ def rank_program(g, core, T, topo):
         if q == "v":
             op("v", lambda: g.vector.memset(out[0], c), [], [out])
         else:
-            act(out, V("one", 0, out[3] - out[2]), AF.Identity, scale=c)
+            act(out, V("one", 0, (out[3] - out[2]) // out[4]), AF.Identity, scale=c)
 
     def quant(q, s, in_):
         op("v", lambda: g.vector.quantize_mx(q[0], s[0], in_[0]), [in_], [q, s])
@@ -233,6 +238,9 @@ def rank_program(g, core, T, topo):
     hi, lo, ends, J = V("hlu", 0, 28), V("hlu", 28, 56), V("se", 2, 4), V("J", 0, 4)
     halves = [(0, HC), (HC, C)]
 
+    def pairs(name, a, e, k):
+        return V(name, ZO + 2 * a + k, ZO + 2 * e + k, 2)
+
     def hb(h, b):
         return bank((4 + 4 * h + b) % 8, HK)
 
@@ -240,22 +248,20 @@ def rank_program(g, core, T, topo):
         return V(name, 128 * b, 128 * b + 128)
 
     def firing(S, t, runs):
-        eq, es, zs = "eq%d" % t, "es%d" % t, V("zs%d" % t)
+        eq, es, zs, mine = "eq%d" % t, "es%d" % t, V("zs%d" % t), V("Lu", 16 * t, 16 * t + 16)
 
         def run(h, a, e):
-            rb, db, cu, s = bank(2 * h, e - a), bank(2 * h + 1, e - a), V("cumb", XO + a, XO + e), str(h)
+            rb, db, cu, rise, s = bank(2 * h, e - a), bank(2 * h + 1, e - a), pairs("cz", a, e, 3), pairs("rz", a, e, 1), str(h)
             S["score" + s] = lambda q: [mm(o, four("uq2", j), four("us2", j), V("xq", a, e), V("xs", a, e)) for j, o in enumerate((rb, db))]
-            S["rise" + s] = lambda q: tt(V("rise", a, e), rb, V("prev", a, e), A.is_gt) if t else ts(V("rise", a, e), rb, 0.0, A.is_gt)
+            S["rise" + s] = lambda q: tt(rise, rb, V("prev", a, e), A.is_gt) if t else ts(rise, rb, 0.0, A.is_gt)
             if t < R - 1:
                 S["prev" + s] = lambda q: lin(q, V("prev", a, e), rb)
-            S["delay" + s] = lambda q: act(V("sgn", a, e), db, AF.Sign, bias=tiny, scale=-1.0)
-            S["count" + s] = lambda q: scan(cu, V("rise", a, e), V("nil", a, e), c1("cumb", XO - 1 + a) if a else -256.0, A.add, A.min)
+            S["delay" + s] = lambda q: act(pairs("rz", a, e, 0), db, AF.Sign, bias=tiny, scale=-1.0)
+            S["count" + s] = lambda q: scan(cu, rise, V("nil", a, e), c1("cz", ZO + 2 * a + 1) if a else -256.0, A.add, A.min)
             S["steps" + s] = lambda q: lin(q, V("cb", a, e), cu, 32.0, kc)
             S["reach" + s] = lambda q: act(V("jnk", a, e), cu, AF.Sign, bias=nthr, acc=c1("acc", 2 + h))
             S["since" + s] = lambda q: scan(V("U", a, e), V("one", a, e), V("cb", a, e), c1("U", a - 1) if a else 0.0, A.add, A.max)
-            S["signed" + s] = lambda q: tt(V("rs", XO + a, XO + e), V("rise", a, e), V("sgn", a, e), A.mult)
-            S["marks" + s] = lambda q: scan(V("vm", XO + a, XO + e, -1), V("cumb", XO - 1 + a, XO - 1 + e, -1), V("rs", XO + a, XO + e, -1),
-                                            0.0, A.min, A.mult)
+            S["marks" + s] = lambda q: scan(*[V(name, ZO + 2 * a, ZO + 2 * e, -1) for name in ("vm", "cz", "rz")], 0.0, A.min, A.mult)
 
         def gather(h, b):
             S["E%d%d" % (h, b)] = lambda q: lin(q, V("E", 4 * HK * h + b, 4 * HK * (h + 1), 4), (state(t), V("eoff", 16 * b + 8 * h, 16 * b + 8 * h + 8)))
@@ -288,12 +294,10 @@ def rank_program(g, core, T, topo):
         S["eoff"] = lambda q: ts(V("eoff"), V("g1"), -4.0, A.mult, 4.0 * C, A.min)
         for h in range(2):
             half(h, HK * h, HK * (h + 1))
-        S["hc"] = lambda q: scan(V("hc"), V("Dg"), V("cumb", XO, XO + C), -256.0, A.add, A.min)
-        S["hp"] = lambda q: scan(V("hp"), V("Dg"), V("cumb", XO - 1, XO - 1 + C), -256.0, A.add, A.min)
-        S["fr"] = lambda q: tt(ls28("fr"), diag("hc"), diag("hp"), A.subtract)
-        S["nf"] = lambda q: lin(q, ls28("nf"), ls28("fr"), -FAR, FAR)
-        S["fP"] = lambda q: lin(q, ls28("fP"), ls28("fr"), float(PW))
-        S["FB"] = lambda q: tt(ls28("FB"), ls28("nf"), ls28("c64"), A.max)
+        S["idle"] = lambda q: act(V("hc"), pairs("vm", 0, C, 1), AF.Sign, bias=c1("cols", 9))
+        S["held"] = lambda q: scan(V("hp"), V("Hm"), V("hc"), 0.0, A.mult, A.add)
+        S["fP"] = lambda q: ts(ls28("fP"), diag("hp"), 0.0, A.is_lt, float(PW), A.mult)
+        S["Lu"] = lambda q: (ts(mine, V("g1", 0, 16), -1.0, A.mult, float(C), A.min), send(mine, V("Ll", 16 * t, 16 * t + 16), "re%d" % t))
         S["sc1"] = lambda q: scan(V("sc1"), V("Dn"), V("vso"), 0.0, A.add, A.min)
         S["r1"] = lambda q: ts(V("r1"), (V("sc1"), ends), 0.0, A.is_ge, FAR, A.mult)
         if t:
@@ -304,8 +308,7 @@ def rank_program(g, core, T, topo):
             S["jt0"] = lambda q: fill(q, V("jt", C, C + 16), -1.0)
             S["jt1"] = lambda q: lin(q, V("jt", 0, C), V("tabI", 0, C), 1.0, 256.0)
         if t == R - 1:
-            S["Lu"] = lambda q: ts(V("Lu"), V("g1", 0, 16), -1.0, A.mult, float(C), A.min)
-            S["ol"] = lambda q: (lin(q, V("olb"), (V("jt"), V("Lu"))), dma("s", "dout", T.ol[:], T.olb[0:128:16, :], [V("olb")], []))
+            S["ol"] = lambda q: (lin(q, V("olb"), (V("jt"), mine)), dma("s", "dout", T.ol[:], T.olb[0:128:16, :], [V("olb")], []))
 
     def merging(S, t):
         lq, ls, zl = "lq%d" % t, "ls%d" % t, ls28("zl%d" % t)
@@ -314,31 +317,35 @@ def rank_program(g, core, T, topo):
             a, e = HK * h, HK * (h + 1)
             out = V("H", 4 * a + b, 4 * e, 4)
             S["relu%d%d" % (h, b)] = lambda q: act(out, hb(h, b), AF.Relu, scale=0.03125) if q == "a" else ts(out, hb(h, b), 0.0, A.max, 0.03125, A.mult)
-            S["half%d%d" % (h, b)] = lambda q: lin(q, cols(slot(t) + PW, a, e, b), hb(h, b), 0.5)
-            c, d = halves[h]
-            o, B = (28 * b + c // 16, 28 * b + d // 16), V("Bb", 4 * c + b, 4 * d, 4)
-            S["B%d%d" % (h, b)] = lambda q: lin(q, B, (state(t), V("oB", *o)), 0.5)
-            S["add%d%d" % (h, b)] = lambda q: tt(cols(xo(t + 1), c, d, b), (V("W", 0, xo(t) + 4 * C), V("oA", *o)), B, A.add)
+            xn = V("Xn", 4 * a + b, 4 * e, 4)
+            S["Xn%d%d" % (h, b)] = lambda q: lin(q, xn, (state(t), V("oN", 64 * t + 16 * b + 8 * h, 64 * t + 16 * b + 8 * h + 8)), 0.5)
+            S["mean%d%d" % (h, b)] = lambda q: tt(cols(slot(t) + PW, a, e, b), hb(h, b), xn, A.add)
+            S["whole%d%d" % (h, b)] = lambda q: lin(q, cols(slot(t), a, e, b), hb(h, b), 2.0)
+            c, d = RUNS[h]
+            S["X%d%d" % (h, b)] = lambda q: lin(q, cols(xo(t + 1), c, d, b), (V("W", 0, xo(t) + 4 * C), V("oA", 28 * b + c // 16, 28 * b + d // 16)))
 
         def half(h):
             a, e = HK * h, HK * (h + 1)
-            c, d = halves[h]
+            c, d = RUNS[h]
+            hq, hs = V("hq", K * t + a, K * t + e), V("hsc", K * t + a, K * t + e)
             S["layer%d" % h] = lambda q: [mm(hb(h, b), four("wl", b), four("wls", b), V(lq, a, e), V(ls, a, e)) for b in range(4)]
-            S["QH%d" % h] = lambda q: (quant(V("hq", a, e), V("hsc", a, e), V("H", 4 * a, 4 * e)),
-                                       [mm(hb(h, b), four("cq", b), four("cs", b), V("hq", a, e), V("hsc", a, e)) for b in range(4)])
-            S["whole%d" % h] = lambda q: lin(q, cols(slot(t), a, e), cols(slot(t) + PW, a, e), 2.0)
+            S["QH%d" % h] = lambda q: (quant(hq, hs, V("H", 4 * a, 4 * e)), [mm(hb(h, b), four("cq", b), four("cs", b), hq, hs) for b in range(4)])
             S["QX%d" % h] = lambda q: quant(V("xq", c, d), V("xs", c, d), cols(xo(t + 1), c, d))
             for b in range(4):
                 element(h, b)
             if t == R - 1:
                 S["y%d" % h] = lambda q: (
-                    mm(bank(h, HC), V("vq"), V("vsc"), V("xq", c, d), V("xs", c, d)),
+                    mm(bank(h, d - c), V("vq"), V("vsc"), V("xq", c, d), V("xs", c, d)),
                     dma("s", "dout", T.oc[:, 4 * c:4 * d], T.xq[:, c:d].bitcast(dt.uint8), [V("xq", c, d)], []),
                     [dma("sa"[k % 2], "dout", T.osc[4 * k:4 * k + 4, :], T.xs[32 * k:32 * k + 4, :], [V("xs")], []) for k in range(4 * h)])
-                S["ys%d" % h] = lambda q: (lin(q, V("ysb", c, d), bank(h, HC)), dma("a", "dout", T.y[:, c:d], T.ysb[:, c:d], [V("ysb", c, d)], []))
+                S["ys%d" % h] = lambda q: (lin(q, V("ysb", c, d), bank(h, d - c)), dma("a", "dout", T.y[:, c:d], T.ysb[:, c:d], [V("ysb", c, d)], []))
 
         def places(b):
-            S["oB%d" % b] = lambda q: ts(V("oB", 28 * b, 28 * b + 28), ls28("q"), float(b), A.add, 4.0 * C, A.min)
+            S["oN%d" % b] = lambda q: ts(V("oN", 64 * t + 16 * b, 64 * t + 16 * b + 16), (V("TK"), c1("LG", 0)), 4.0, A.mult, 4.0 * K + b, A.add)
+            if t:
+                old = V("Xo", b, 4 * K, 4)
+                S["Xo%d" % b] = lambda q: lin(q, old, (state(t), V("oN", 64 * (t - 1) + 16 * b, 64 * (t - 1) + 16 * b + 16)), 0.5)
+                S["meano%d" % b] = lambda q: tt(cols(slot(t - 1) + PW, 0, K, b), bank(4 + b, K), old, A.add)
             S["oA%d" % b] = lambda q: ts(V("oA", 28 * b, 28 * b + 28), ls28("mc"), float(slot(t + 1) + b), A.add)
 
         if t < R - 1:
@@ -347,7 +354,11 @@ def rank_program(g, core, T, topo):
             S["r4"] = lambda q: lin(q, V("r4"), (V("sc2"), ends), -1.0, -4.0 * K)
             S["Bt"] = lambda q: tt(V("Bt"), V("r4"), V("r3"), A.add)
         S["own"] = lambda q: lin(q, ls28("own"), ls28("c64"), 1.0, float(xo(t) - slot(t + 1)))
-        S["q"] = lambda q: tt(ls28("q"), zl, ls28("FB"), A.max)
+        S["tk"] = lambda q: lin(q, V("tk", 16, 16 + K), (V("trow"), V("Ll", 16 * t, 16 * t + 16)))
+        S["tu0"] = lambda q: turn(V("TK", 0, K), V("tk", 16, 16 + K))
+        S["tu1"] = lambda q: turn(V("TK", K, 2 * K + 32), V("tk"))
+        if t:
+            S["again"] = lambda q: [mm(bank(4 + b, K), four("cq", b), four("cs", b), V("hq", K * (t - 1), K * t), V("hsc", K * (t - 1), K * t)) for b in range(4)]
         S["mb"] = lambda q: tt(ls28("mb"), zl, ls28("fP"), A.add)
         S["mc"] = lambda q: tt(ls28("mc"), ls28("mb"), ls28("own"), A.min)
         for k in range(4):
@@ -381,15 +392,15 @@ def rank_program(g, core, T, topo):
                     ("s16", [[0, 16], [16, 2]], 0, 0), ("sdat", [[32, 14], [0, 2], [1, 16]], -255, 0)):
             counted(*row)
         for row in (("sw0", V("swin", 0, SL), -256.0), ("sw1", V("swin", SL, 2 * SL), -256.0), ("nil", V("nil"), 0.0), ("tiny", tiny, 2.0 ** -110),
-                    ("pre0", V("pre", 0, 4), 2.0 - C), ("cu0", V("cumb", 0, XO), -256.0), ("vmz", V("vm", 0, XO), 0.0),
-                    ("mj0", V("maskJ", 0, XO), ASIDE), ("ms0", V("maskS", 0, XO), ASIDE), ("big", V("big"), 2.0 ** 20)):
+                    ("pre0", V("pre", 0, 4), 2.0 - C), ("cu0", c1("cz", ZO + 1), -256.0), ("cu1", pairs("cz", 0, C, 0), ASIDE), ("vmz", V("vm", 0, ZO), 0.0),
+                    ("mj0", V("maskJ", 0, ZO), ASIDE), ("ms0", V("maskS", 0, XO), ASIDE), ("big", V("big"), 2.0 ** 20), ("hf", c1("cols", 9), 0.5)):
             filled(*row)
         for row in (("k0", k0, fi, 2050.0, 32768.0), ("kc", kc, fi, -32.0, STEP + 32 * 263.5), ("nthr", nthr, fi, -16.0, 239.5),
                     ("f4", f4, fi, 4.0), ("r16", r16, fs, 16.0), ("c64", V("c64"), V("h16"), 4.0, f4),
                     ("cm", V("cm"), V("cm"), 0.25), ("sdat", V("sdat"), V("sdat"), 1.0, r16),
                     ("tF1", V("tabF", 16, 32), V("tabF", 0, 16), 1024.0), ("tM0", V("tabM", 0, 16), V("tabF", 0, 16), 1.0),
                     ("tM1", V("tabM", 16, 32), V("tabF", 0, 16), 2.0 ** -10), ("init", init, c1("acc", 0), 1.0, k0),
-                    ("Fr", V("Fr"), (V("tabF"), hi), 1.0), ("maskJ", V("maskJ", XO, XO + C), (V("tabF", 0, 16), lo), ASIDE),
+                    ("Fr", V("Fr"), (V("tabF"), hi), 1.0), ("maskJ", pairs("maskJ", 0, C, 0), (V("tabF", 0, 16), lo), ASIDE), ("fib", c1("fib", 0), fi, 1.0),
                     ("Dp", V("Dp"), V("Dn"), -1.0)):
             scaled(*row)
         for k in range(2):
@@ -398,7 +409,16 @@ def rank_program(g, core, T, topo):
             unpacking(b)
         S["one"] = lambda q: fill("v", V("one"), 1.0)
         S["pad"] = lambda q: fill("v", V("W", xo(0) + 4 * C, xo(R), RX), 0.0)
-        S["Z"] = lambda q: op("p", lambda: g.affine_select(T.Z[:], T.one[:], [[-1, 528]], A.is_equal, 0.0, 3, 4), [V("one")], [V("Z")])
+        S["Z"] = lambda q: op("p", lambda: g.affine_select(T.Z[:], T.nil[:], [[-1, 528]], A.not_equal, 0.5, 3, 4), [V("nil")], [V("Z")])
+        S["ip17"] = lambda q: iota(V("ib", 4, 8), [[0, 4]], 0, 17)
+        S["ci2"] = lambda q: ts(c1("ci", 2), c1("ib", 4), 4, A.arith_shift_right, 1, A.bitwise_and)
+        S["fx"] = lambda q: cp(c1("cols", 10), c1("ci", 2))
+        S["i16"] = lambda q: lin(q, c1("cols", 11), fi, 16.0)
+        S["LG"] = lambda q: ts(c1("LG", 0), c1("cols", 10), 272.0, A.mult, c1("cols", 11), A.add)
+        S["tgu"] = lambda q: (cp(ls28("tgu"), ls28("tgi")), send(ls28("tgu"), ls28("tgl"), "rt"))
+        S["trow"] = lambda q: lin(q, V("trow", 0, C), (V("tabI"), ls28("tgl")))
+        S["tr0"] = lambda q: fill(q, V("trow", C, C + 16), -256.0)
+        S["tk0"] = lambda q: fill(q, V("tk"), 0.0)
         S["ci0"] = lambda q: ts(c1("ci", 0), c1("pint", 0), 15, A.bitwise_and)
         S["ci1"] = lambda q: ts(c1("ci", 1), c1("pint", 0), 4, A.arith_shift_right, 1, A.bitwise_and)
         S["fi"] = lambda q: cp(V("cols", 0, 2), V("ci", 0, 2))
@@ -408,7 +428,7 @@ def rank_program(g, core, T, topo):
         S["up0"] = lambda q: cp(V("upo", 0, 8), V("h16", 0, 8))
         S["up1"] = lambda q: ts(V("upo", 8, 16), V("h16", 0, 8), 1.0, A.add)
         S["segrow"] = lambda q: act(V("segrow"), V("jj"), AF.Sign)
-        S["Dg"] = lambda q: ts(V("Dg"), V("jj"), fi, A.is_equal, 1024.0, A.mult)
+        S["Hm"] = lambda q: ts(V("Hm"), V("jj"), c1("fib", 0), A.not_equal, 2.0, A.mult)
         S["Qu"] = lambda q: quant(V("uq"), V("us"), V("ut"))
         S["sendW"] = lambda q: (send(V("wq"), V("wl"), "rw", codes=True), send(V("wsc"), V("wls"), "rw"))
         S["hi"] = lambda q: ts(V("hl", 0, 28), ls28("tgi"), 4, A.arith_shift_right)
@@ -433,7 +453,7 @@ def rank_program(g, core, T, topo):
         S["scatter"] = lambda q: scatter(V("swin"), ls28("spos"), V("sdat"))
         S["ST"] = lambda q: turn(V("ST"), V("swin"))
         S["sg"] = lambda q: tt(V("sg"), V("ST", 0, 2 * SL, 32), V("ST", 16, 2 * SL, 32), A.add)
-        S["sig"] = lambda q: ts(V("sig"), V("sg"), 512.0 + XO - 1, A.add)
+        S["sig"] = lambda q: ts(V("sig"), V("sg"), 2.0, A.mult, ZO + 1022.0, A.add)
         S["Dn"] = lambda q: tt(V("Dn"), (V("maskJ"), V("sig")), V("maskS", XO - 1, XO + SL - 1), A.subtract)
         S["open"] = lambda q: scatter(V("Dn"), V("se", 0, 2), V("big"))
 
@@ -445,7 +465,9 @@ def rank_program(g, core, T, topo):
     dma("s", "dw", T.wsc[:], T.ws[:], [], [V("wsc")])
     dma("s", "dv", T.vt[:], T.v[:], [], [V("vt")])
     landed("rw", 2 * ne, [V("wl"), V("wls")])
+    landed("rt", ne, [V("tgl")])
     for t in range(R):
+        landed("re%d" % t, ne, [V("Ll", 16 * t, 16 * t + 16)])
         landed("rl%d" % t, ne, [V("zl%d" % t)])
         landed("rc%d0" % t, 2 * ne, [V("lq%d" % t, 0, HK), V("ls%d" % t)])
         landed("rc%d1" % t, ne, [V("lq%d" % t, HK, K)])
@@ -453,7 +475,7 @@ def rank_program(g, core, T, topo):
     steps = [{} for _ in range(R + 1)]
     starting(steps[0])
     for t in range(R):
-        firing(steps[t], t, halves if t else [(0, C)])
+        firing(steps[t], t, RUNS if t else [(0, C)])
         merging(steps[t + 1], t)
     for t, order in enumerate([START] + [ROUND] * (R - 1) + [END]):
         for word in order.split():

from concourse.mybir import dt, AluOpType, ActivationFunctionType

C, K, R = 448, 256, 3
HC = C // 2
HK = K // 2
RUNS = [(0, 256), (256, C)]
XO = 16
ZO = 16
RX = 4 * C + 16
PW = R * 4 * K
FAR = 32768.0
STEP = 65536.0
ASIDE = 4096.0
SL = 512
F32, BF, I32, U16, U8, MX = "float32", "bfloat16", "int32", "uint16", "uint8", "float8_e4m3fn_x4"

START = """
    one nil:v pre0:a ipint cu0:v ih16 ci1 ci0 ihh fi pad k0:v tB1 up0 tF0 hi tk0:v lo sw1:a cu1:a tF1:v ijj icm tB0 is16
    fib:a hlu Qu tM1:v tM0:a acc up1 Hm uq1 QX0 uq0 Z us0 isdat Fr:a cq0 mj0:v r16:a tgu ip17 us1 cm:a i16:a nthr:a
    init:v QX1 f4:a kc:a score0 itabI c64:a cum segrow hf:a ib0 rise0 prev0:a val count0 T1 sw0:a ms0:a ci2 reach0
    steps0:a tiny:v seg J fx a0 sdat:a vmz:a since0 a1 g2 delay0 maskJ:a ib1 a2 a3 g1 a4 LG sendW eoff
    E02:a E03:a spos cq1 scatter E01:a Lu E00:a E13:a ob0 E12:a QE0 E11:a ST ob1 sg E10:a tr0:a QE1 sig +own:a trow:a
    maskS0:a marks0 vso0:a maskS1:v se Dn +jt0:a big:a cq3 open vso1:a sc1 cq2 +tk:a r1 idle Dp:a +Qv zs
    +tu1 +layer0 +tu0 held +oN3 +relu00:a +oN1 +relu01:a +relu02:a +layer1 +sc2 +relu03:a +QH0 +Xn03:a +relu10:a +oN2
    +relu13:a +oN0 +relu12:a +relu11:v +Xn01:v +Xn11:a +whole02:a +r3 +Xn12:a +QH1 +Xn02:v +whole00:v fP +mean02
    +Xn10:a +mean01 +mean10 +mean03 +Xn00:a +whole13:v +mean12 +Xn13:a +mean11 +whole10:a +mb +mean00 +whole01:a +mc
    +r4:a +whole12:a +mean13 +oA1 +whole03:a +oA3 +oA0 +Bt +whole11:a +oA2"""
ROUND = """
    X01:a X00:v X02:a X10:a X13:a X03:v QX0 score0 X11:a delay0 X12:v rise0 QX1 count0 score1 rise1 count1 prev0:a
    marks0 reach0 steps0:a pre:a delay1 since0 reach1 marks1 +own:v J steps1:a since1 +Xo0:a vso0:a g2 vso1:a g1 eoff Lu
    E02:a E03:a E12:a +again E11:v E01:v E00:v E10:a E13:v QE0 sc1 QE1
    +Xo1:a r1 +Xo3:v r2 idle +meano0 zs +Xo2:a held +tk:a +meano1 +meano3 +tu1 jt1:a +tu0 +meano2 +oN2 fP +oN0
    +layer0 prev1:a +layer1 +Xn02:a +oN1 +sc2 +oN3 +Xn12:v +Xn01:a +Xn00:a +Xn03:v +Xn13:a
    +relu00:v +relu01:a +relu02:v +relu03:v +mb +relu10:a +QH0 +relu11:a +relu13:v +r3 +relu12:a +r4:a +mc +QH1
    +mean00 +whole02:v +Xn11:a +mean03 +Xn10:a +oA1 +whole00:a +whole10:a +mean11 +whole12:a +mean01 +mean02 +mean10
    +mean12 +whole13:a +mean13 +whole03:a +oA0 +whole01:a +whole11:a +oA2 +Bt +oA3"""
END = """
    X01:a X00:v X03:a X02:v QX0 y0 X13:a X10:v X11:a X12:v QX1 ys0:a y1 -ol:v ys1:a"""

SCRATCH = {"ps": ("psum", [128, 4096], F32)}
for _d, _bufs in (
    (BF, {"W": 2 * PW + (R + 1) * RX, "ut": 512, "vt": 512, "one": 528, "Z": 528, "cz": 2 * (ZO + C), "rz": 2 * (ZO + C), "cb": C,
          "Xn": 4 * K, "Xo": 4 * K, "trow": C + 16, "tk": K + 32, "TK": 2 * K + 32, "nil": 528, "jj": C, "Hm": C, "hc": C, "hp": C, "jnk": C, "big": 32, "fib": 16,
          "E": 4 * K, "H": 4 * K, "tabI": 528, "sdat": C, "segrow": C, "swin": 2 * SL, "ST": 2 * SL, "Dn": SL, "Dp": SL,
          "maskJ": 2 * (ZO + C), "maskS": XO + SL, "vm": 2 * (ZO + C), "vso": SL, "sc1": SL, "sc2": SL}),
    (MX, {"xq": C, "uq": 128, "uq2": 256, "vq": 128, "wq": 512, "wl": 512, "hq": R * K, "cq": 512,
          "eq0": K, "eq1": K, "eq2": K, "lq0": K, "lq1": K, "lq2": K}),
    (U8, {"xs": C, "us": 128, "us2": 256, "vsc": 128, "wsc": 512, "wls": 512, "hsc": R * K, "cs": 512,
          "es0": K, "es1": K, "es2": K, "ls0": K, "ls1": K, "ls2": K}),
    (F32, {"prev": C, "ysb": C, "olb": K, "cols": 16, "h16": 32, "hh": 16, "c64": 32, "cm": 64,
           "tabF": 32, "tabM": 32, "tabB": 32, "Fr": C, "acc": 8, "cum": C, "val": C, "T1": C, "seg": C, "sg": 32,
           "U": C, "jt": C + 16, "pre": 8, "g1": 64, "g2": 64, "fP": 32,
           "r1": 32, "r2": 32, "r3": 32, "r4": 32, "mc": 32, "own": 32,
           "Bt": 32, "mb": 32, "zs0": 32, "zs1": 32, "zs2": 32, "zl0": 32, "zl1": 32, "zl2": 32}),
    (I32, {"pint": 8, "ci": 8, "s16": 32, "tgi": 32, "hl": 56, "a0": 32, "a1": 32, "a2": 32, "a3": 32, "ib": 8, "ob": 8}),
    (U16, {"eoff": 64, "upo": 16, "J": 8, "Lu": 16 * R, "Ll": 16 * R, "tgu": 32, "tgl": 32, "LG": 2, "oN": 64 * R,
           "hlu": 56, "spos": 32, "sig": 32, "se": 8, "oA": 128}),
):
    for _k in _bufs:
        SCRATCH[_k] = ("sbuf", [128, _bufs[_k]], _d)

SEMAPHORES = (["sv", "sa", "st", "sp", "sent", "dtg", "du", "dx0", "dx1", "dw", "dv", "dout", "rw", "rt"]
              + ["rc%d%d" % (_t, _h) for _t in range(R) for _h in range(2)] + ["r%s%d" % (_k, _t) for _k in "le" for _t in range(R)])


def xo(t):
    return 2 * PW + RX * t


def slot(t):
    return 4 * K * t


def rank_program(g, core, T, topo):
    rank = T.rank_of(core)
    if rank is None:
        return
    n = len(T.cores)
    dst = T.cores[(rank + 1) % n]
    rid, pid = topo.addr(dst)[0], topo.addr(dst)[1]
    mask = topo.mask(core, dst)
    ne = len(topo.engines(core, dst))
    A, AF = AluOpType, ActivationFunctionType

    Q = {"v": g.vector, "a": g.scalar, "t": g.tensor, "p": g, "s": g.sync}
    own = {"v": "sv", "a": "sa", "t": "st", "p": "sp"}
    cnt = {}
    known = {q: {} for q in Q}
    log = {}

    def V(name, a=0, b=None, step=1):
        b = SCRATCH[name][1][1] if b is None else b
        if step < 0:
            return (T[name][:, b - 1:a - 1:-1], name, a, b, 1)
        view = T[name][:, a:b:step] if step > 1 else T[name][:, a:b]
        if name == "ps":
            return (view, name, a // 512 * 512, (b + 511) // 512 * 512, 1)
        return (view, name, a, b, step)

    def meet(x, y):
        if x[3] <= y[2] or y[3] <= x[2]:
            return False
        return not (x[4] == y[4] and x[4] > 1 and (x[2] - y[2]) % x[4] != 0)

    def wait(q, sem, val, clock):
        if known[q].get(sem, 0) < val:
            Q[q].wait_ge(T.sem[sem], val)
            known[q][sem] = val
            for s in clock:
                if known[q].get(s, 0) < clock[s]:
                    known[q][s] = clock[s]

    def before(q, reads, writes):
        need = []
        for v, wr in [(r, False) for r in reads] + [(w, True) for w in writes]:
            for (u, uw, uq, tok) in log.get(v[1], []):
                if (wr or uw or (v[1] == "ps" and uq != q)) and meet(u, v):
                    need.append(tok)
        need.sort(key=lambda k: -k[1])
        for sem, val, clock in need:
            wait(q, sem, val if sem in own.values() else cnt[sem], clock)

    def after(q, reads, writes, sem):
        tok = (sem, cnt[sem], dict(known[q]))
        for v, wr in [(r, False) for r in reads] + [(w, True) for w in writes]:
            log.setdefault(v[1], []).append((v, wr, q, tok))

    def op(q, call, reads, writes):
        before(q, reads, writes)
        sem = own[q]
        call().then_inc(T.sem[sem], 1)
        cnt[sem] = cnt.get(sem, 0) + 1
        after(q, reads, writes, sem)

    def dma(q, sem, out, in_, reads, writes):
        before(q, reads, writes)
        Q[q].dma_start(out, in_).then_inc(T.sem[sem], 16)
        cnt[sem] = cnt.get(sem, 0) + 16
        after(q, reads, writes, sem)

    def landed(sem, val, writes):
        cnt[sem] = val
        for w in writes:
            log.setdefault(w[1], []).append((w, True, "far", (sem, val, {})))

    def send(src, out, sem, codes=False):
        before("p", [src], [])
        a, b = (out[0].bitcast(dt.uint8), src[0].bitcast(dt.uint8)) if codes else (out[0], src[0])
        g.remote_dma(a, b, T.sem[sem], T.sem["sent"], pid, rid, mask)
        cnt["sent"] = cnt.get("sent", 0) + ne

    def ap(x):
        return x[0][0].indirect(x[1][0]) if len(x) == 2 else x[0]

    def vs(x):
        return [x[0], x[1]] if len(x) == 2 else [x]

    def num(x):
        return isinstance(x, (int, float)) or x is None

    def ts(out, in0, s1, op0, s2=None, op1=None):
        rd = vs(in0) + [s for s in (s1, s2) if not num(s)]
        x1, x2 = (s1 if num(s1) else s1[0]), (s2 if num(s2) else s2[0])
        if op1 is None:
            op("v", lambda: g.vector.tensor_scalar(out[0], ap(in0), x1, None, op0), rd, [out])
        else:
            op("v", lambda: g.vector.tensor_scalar(out[0], ap(in0), x1, x2, op0, op1), rd, [out])

    def tt(out, in0, in1, o):
        op("v", lambda: g.vector.tensor_tensor(out[0], ap(in0), in1[0], o), vs(in0) + [in1], [out])

    def cp(out, in_):
        op("v", lambda: g.vector.tensor_copy(out[0], ap(in_)), vs(in_), [out])

    def scatter(win, off, in_):
        op("v", lambda: g.vector.tensor_copy(win[0].indirect(off[0]), in_[0]), [off, in_], [win])

    def scan(out, d0, d1, init, op0, op1):
        rd = [d0, d1] + ([] if num(init) else [init])
        op("v", lambda: g.vector.tensor_tensor_scan(out[0], d0[0], d1[0], init if num(init) else init[0], op0, op1), rd, [out])

    def turn(out, in_):
        op("v", lambda: g.vector.transpose(out[0], in_[0]), [in_], [out])

    def act(out, in_, func, bias=0.0, scale=1.0, acc=None):
        rd = vs(in_) + [s for s in (bias, scale) if not num(s)]
        b, s = (bias if num(bias) else bias[0]), (scale if num(scale) else scale[0])
        if acc is None:
            op("a", lambda: g.scalar.activation(out[0], ap(in_), func, bias=b, scale=s), rd, [out])
        else:
            op("a", lambda: g.scalar.activation(out[0], ap(in_), func, bias=b, scale=s, accum_out=acc[0]), rd, [out, acc])

    def lin(q, out, in_, scale=1.0, bias=0.0):
        if q == "a":
            act(out, in_, AF.Identity, bias, scale)
        elif num(bias) and scale == 1.0 and bias == 0.0:
            cp(out, in_)
        else:
            ts(out, in_, scale, A.mult, bias, A.add)

    def fill(q, out, c):
        if q == "v":
            op("v", lambda: g.vector.memset(out[0], c), [], [out])
        else:
            act(out, V("one", 0, (out[3] - out[2]) // out[4]), AF.Identity, scale=c)

    def quant(q, s, in_):
        op("v", lambda: g.vector.quantize_mx(q[0], s[0], in_[0]), [in_], [q, s])

    def mm(out, wq, ws, xq, xs):
        op("t", lambda: g.tensor.matmul_mx(out[0], wq[0], ws[0], xq[0], xs[0], True, True), [wq, ws, xq, xs], [out])

    def iota(out, pattern, base, cm):
        if SCRATCH[out[1]][2] == I32:
            op("p", lambda: g.iota(out[0], pattern, base, cm), [], [out])
        else:
            op("p", lambda: g.iota(out[0], pattern, base, cm, allow_small_or_imprecise_dtypes=True), [], [out])

    def bank(b, w):
        return V("ps", 512 * b, 512 * b + w)

    def c1(name, j):
        return V(name, j, j + 1)

    def cols(base, a, e, b=None):
        return V("W", base + 4 * a, base + 4 * e) if b is None else V("W", base + 4 * a + b, base + 4 * e, 4)

    def state(t):
        return V("W", xo(t), xo(t) + RX)

    def ls28(name):
        return V(name, 0, 28)

    def diag(name):
        return V(name, 15, C, 16)

    fi, fs, kc, nthr, k0, r16, init, f4, tiny = [c1("cols", j) for j in range(9)]
    hi, lo, ends, J = V("hlu", 0, 28), V("hlu", 28, 56), V("se", 2, 4), V("J", 0, 4)
    halves = [(0, HC), (HC, C)]

    def pairs(name, a, e, k):
        return V(name, ZO + 2 * a + k, ZO + 2 * e + k, 2)

    def hb(h, b):
        return bank((4 + 4 * h + b) % 8, HK)

    def four(name, b):
        return V(name, 128 * b, 128 * b + 128)

    def firing(S, t, runs):
        eq, es, zs, mine = "eq%d" % t, "es%d" % t, V("zs%d" % t), V("Lu", 16 * t, 16 * t + 16)

        def run(h, a, e):
            rb, db, cu, rise, s = bank(2 * h, e - a), bank(2 * h + 1, e - a), pairs("cz", a, e, 3), pairs("rz", a, e, 1), str(h)
            S["score" + s] = lambda q: [mm(o, four("uq2", j), four("us2", j), V("xq", a, e), V("xs", a, e)) for j, o in enumerate((rb, db))]
            S["rise" + s] = lambda q: tt(rise, rb, V("prev", a, e), A.is_gt) if t else ts(rise, rb, 0.0, A.is_gt)
            if t < R - 1:
                S["prev" + s] = lambda q: lin(q, V("prev", a, e), rb)
            S["delay" + s] = lambda q: act(pairs("rz", a, e, 0), db, AF.Sign, bias=tiny, scale=-1.0)
            S["count" + s] = lambda q: scan(cu, rise, V("nil", a, e), c1("cz", ZO + 2 * a + 1) if a else -256.0, A.add, A.min)
            S["steps" + s] = lambda q: lin(q, V("cb", a, e), cu, 32.0, kc)
            S["reach" + s] = lambda q: act(V("jnk", a, e), cu, AF.Sign, bias=nthr, acc=c1("acc", 2 + h))
            S["since" + s] = lambda q: scan(V("U", a, e), V("one", a, e), V("cb", a, e), c1("U", a - 1) if a else 0.0, A.add, A.max)
            S["marks" + s] = lambda q: scan(*[V(name, ZO + 2 * a, ZO + 2 * e, -1) for name in ("vm", "cz", "rz")], 0.0, A.min, A.mult)

        def gather(h, b):
            S["E%d%d" % (h, b)] = lambda q: lin(q, V("E", 4 * HK * h + b, 4 * HK * (h + 1), 4), (state(t), V("eoff", 16 * b + 8 * h, 16 * b + 8 * h + 8)))

        def half(h, a, e):
            def pack(q):
                quant(V(eq, a, e), V(es, a, e), V("E", 4 * a, 4 * e))
                if h:
                    send(V(es), V("ls%d" % t), "rc%d0" % t)
                send(V(eq, a, e), V("lq%d" % t, a, e), "rc%d%d" % (t, h), codes=True)
            S["QE%d" % h] = pack
            S["vso%d" % h] = lambda q: lin(q, V("vso", 256 * h, 256 * h + 256), (V("vm"), V("sig", 16 * h, 16 * h + 16)), 4.0)
            for b in range(4):
                gather(h, b)

        def winners(q):
            if t:
                tt(zs, V("r2"), V("Bt"), A.min)
            else:
                tt(zs, (V("sc1"), ends), V("r1"), A.add)
            send(zs, V("zl%d" % t), "rl%d" % t)

        for h, (a, e) in enumerate(runs):
            run(h, a, e)
        if len(runs) == 2:
            S["pre"] = lambda q: lin(q, V("pre", 4, 8), V("pre", 0, 4), 1.0, c1("acc", 2))
        S["J"] = lambda q: ts(J, V("pre", 4 * len(runs) - 4, 4 * len(runs)), c1("acc", 1 + len(runs)), A.add, -0.5, A.mult)
        S["g2"] = lambda q: tt(V("g2"), (V("tabI"), J), V("cm"), A.add)
        S["g1"] = lambda q: tt(V("g1"), (V("U"), J), V("g2"), A.subtract)
        S["eoff"] = lambda q: ts(V("eoff"), V("g1"), -4.0, A.mult, 4.0 * C, A.min)
        for h in range(2):
            half(h, HK * h, HK * (h + 1))
        S["idle"] = lambda q: act(V("hc"), pairs("vm", 0, C, 1), AF.Sign, bias=c1("cols", 9))
        S["held"] = lambda q: scan(V("hp"), V("Hm"), V("hc"), 0.0, A.mult, A.add)
        S["fP"] = lambda q: ts(ls28("fP"), diag("hp"), 0.0, A.is_lt, float(PW), A.mult)
        S["Lu"] = lambda q: (ts(mine, V("g1", 0, 16), -1.0, A.mult, float(C), A.min), send(mine, V("Ll", 16 * t, 16 * t + 16), "re%d" % t))
        S["sc1"] = lambda q: scan(V("sc1"), V("Dn"), V("vso"), 0.0, A.add, A.min)
        S["r1"] = lambda q: ts(V("r1"), (V("sc1"), ends), 0.0, A.is_ge, FAR, A.mult)
        if t:
            S["r2"] = lambda q: tt(V("r2"), (V("sc1"), ends), V("r1"), A.add)
        S["zs"] = winners
        if t == 1:
            S["Qv"] = lambda q: quant(V("vq"), V("vsc"), V("vt"))
            S["jt0"] = lambda q: fill(q, V("jt", C, C + 16), -1.0)
            S["jt1"] = lambda q: lin(q, V("jt", 0, C), V("tabI", 0, C), 1.0, 256.0)
        if t == R - 1:
            S["ol"] = lambda q: (lin(q, V("olb"), (V("jt"), mine)), dma("s", "dout", T.ol[:], T.olb[0:128:16, :], [V("olb")], []))

    def merging(S, t):
        lq, ls, zl = "lq%d" % t, "ls%d" % t, ls28("zl%d" % t)

        def element(h, b):
            a, e = HK * h, HK * (h + 1)
            out = V("H", 4 * a + b, 4 * e, 4)
            S["relu%d%d" % (h, b)] = lambda q: act(out, hb(h, b), AF.Relu, scale=0.03125) if q == "a" else ts(out, hb(h, b), 0.0, A.max, 0.03125, A.mult)
            xn = V("Xn", 4 * a + b, 4 * e, 4)
            S["Xn%d%d" % (h, b)] = lambda q: lin(q, xn, (state(t), V("oN", 64 * t + 16 * b + 8 * h, 64 * t + 16 * b + 8 * h + 8)), 0.5)
            S["mean%d%d" % (h, b)] = lambda q: tt(cols(slot(t) + PW, a, e, b), hb(h, b), xn, A.add)
            S["whole%d%d" % (h, b)] = lambda q: lin(q, cols(slot(t), a, e, b), hb(h, b), 2.0)
            c, d = RUNS[h]
            S["X%d%d" % (h, b)] = lambda q: lin(q, cols(xo(t + 1), c, d, b), (V("W", 0, xo(t) + 4 * C), V("oA", 28 * b + c // 16, 28 * b + d // 16)))

        def half(h):
            a, e = HK * h, HK * (h + 1)
            c, d = RUNS[h]
            hq, hs = V("hq", K * t + a, K * t + e), V("hsc", K * t + a, K * t + e)
            S["layer%d" % h] = lambda q: [mm(hb(h, b), four("wl", b), four("wls", b), V(lq, a, e), V(ls, a, e)) for b in range(4)]
            S["QH%d" % h] = lambda q: (quant(hq, hs, V("H", 4 * a, 4 * e)), [mm(hb(h, b), four("cq", b), four("cs", b), hq, hs) for b in range(4)])
            S["QX%d" % h] = lambda q: quant(V("xq", c, d), V("xs", c, d), cols(xo(t + 1), c, d))
            for b in range(4):
                element(h, b)
            if t == R - 1:
                S["y%d" % h] = lambda q: (
                    mm(bank(h, d - c), V("vq"), V("vsc"), V("xq", c, d), V("xs", c, d)),
                    dma("s", "dout", T.oc[:, 4 * c:4 * d], T.xq[:, c:d].bitcast(dt.uint8), [V("xq", c, d)], []),
                    [dma("sa"[k % 2], "dout", T.osc[4 * k:4 * k + 4, :], T.xs[32 * k:32 * k + 4, :], [V("xs")], []) for k in range(4 * h)])
                S["ys%d" % h] = lambda q: (lin(q, V("ysb", c, d), bank(h, d - c)), dma("a", "dout", T.y[:, c:d], T.ysb[:, c:d], [V("ysb", c, d)], []))

        def places(b):
            S["oN%d" % b] = lambda q: ts(V("oN", 64 * t + 16 * b, 64 * t + 16 * b + 16), (V("TK"), c1("LG", 0)), 4.0, A.mult, 4.0 * K + b, A.add)
            if t:
                old = V("Xo", b, 4 * K, 4)
                S["Xo%d" % b] = lambda q: lin(q, old, (state(t), V("oN", 64 * (t - 1) + 16 * b, 64 * (t - 1) + 16 * b + 16)), 0.5)
                S["meano%d" % b] = lambda q: tt(cols(slot(t - 1) + PW, 0, K, b), bank(4 + b, K), old, A.add)
            S["oA%d" % b] = lambda q: ts(V("oA", 28 * b, 28 * b + 28), ls28("mc"), float(slot(t + 1) + b), A.add)

        if t < R - 1:
            S["sc2"] = lambda q: scan(V("sc2"), V("Dp"), V("vso"), 0.0, A.add, A.max)
            S["r3"] = lambda q: ts(V("r3"), (V("sc2"), ends), 0.0, A.is_le, FAR, A.mult)
            S["r4"] = lambda q: lin(q, V("r4"), (V("sc2"), ends), -1.0, -4.0 * K)
            S["Bt"] = lambda q: tt(V("Bt"), V("r4"), V("r3"), A.add)
        S["own"] = lambda q: lin(q, ls28("own"), ls28("c64"), 1.0, float(xo(t) - slot(t + 1)))
        S["tk"] = lambda q: lin(q, V("tk", 16, 16 + K), (V("trow"), V("Ll", 16 * t, 16 * t + 16)))
        S["tu0"] = lambda q: turn(V("TK", 0, K), V("tk", 16, 16 + K))
        S["tu1"] = lambda q: turn(V("TK", K, 2 * K + 32), V("tk"))
        if t:
            S["again"] = lambda q: [mm(bank(4 + b, K), four("cq", b), four("cs", b), V("hq", K * (t - 1), K * t), V("hsc", K * (t - 1), K * t)) for b in range(4)]
        S["mb"] = lambda q: tt(ls28("mb"), zl, ls28("fP"), A.add)
        S["mc"] = lambda q: tt(ls28("mc"), ls28("mb"), ls28("own"), A.min)
        for k in range(4):
            places(k)
        for h in range(2):
            half(h)

    def starting(S):
        def counted(name, pattern, base, cm):
            S["i" + name] = lambda q: iota(V(name), pattern, base, cm)

        def filled(name, out, c):
            S[name] = lambda q: fill(q, out, c)

        def scaled(name, out, in_, scale, bias=0.0):
            S[name] = lambda q: lin(q, out, in_, scale, bias)

        def each(k):
            o = V("upo", 8 * k, 8 * k + 8)
            S["us%d" % k] = lambda q: op("a", lambda: g.scalar.activation(four("us2", k)[0], T.us[:].indirect(o[0]), AF.Copy), [V("us"), o], [four("us2", k)])
            S["uq%d" % k] = lambda q: op("v", lambda: g.vector.tensor_copy(four("uq2", k)[0].bitcast(dt.uint32), T.uq[:].bitcast(dt.uint32).indirect(o[0])),
                                         [V("uq"), o], [four("uq2", k)])
            scaled("maskS%d" % k, V("maskS", XO + 256 * k, XO + 256 * k + 256), (V("maskJ"), V("sig", 16 * k, 16 * k + 16)), 1.0)
            S["QX%d" % k] = lambda q: quant(V("xq", *halves[k]), V("xs", *halves[k]), cols(xo(0), *halves[k]))

        def unpacking(b):
            S["cq%d" % b] = lambda q: quant(four("cq", b), four("cs", b), V("Z", 3 - b, 515 - b))

        for row in (("pint", [[0, 8]], 0, 1), ("hh", [[1, 16]], 0, 0), ("h16", [[16, 32]], 0, 0), ("jj", [[0, 28], [1, 16]], 0, 0),
                    ("tabI", [[1, 528]], -256, 0), ("cm", [[1, 4], [2048, 16]], 4 * (int(STEP) + 512 + 256), 0),
                    ("s16", [[0, 16], [16, 2]], 0, 0), ("sdat", [[32, 14], [0, 2], [1, 16]], -255, 0)):
            counted(*row)
        for row in (("sw0", V("swin", 0, SL), -256.0), ("sw1", V("swin", SL, 2 * SL), -256.0), ("nil", V("nil"), 0.0), ("tiny", tiny, 2.0 ** -110),
                    ("pre0", V("pre", 0, 4), 2.0 - C), ("cu0", c1("cz", ZO + 1), -256.0), ("cu1", pairs("cz", 0, C, 0), ASIDE), ("vmz", V("vm", 0, ZO), 0.0),
                    ("mj0", V("maskJ", 0, ZO), ASIDE), ("ms0", V("maskS", 0, XO), ASIDE), ("big", V("big"), 2.0 ** 20), ("hf", c1("cols", 9), 0.5)):
            filled(*row)
        for row in (("k0", k0, fi, 2050.0, 32768.0), ("kc", kc, fi, -32.0, STEP + 32 * 263.5), ("nthr", nthr, fi, -16.0, 239.5),
                    ("f4", f4, fi, 4.0), ("r16", r16, fs, 16.0), ("c64", V("c64"), V("h16"), 4.0, f4),
                    ("cm", V("cm"), V("cm"), 0.25), ("sdat", V("sdat"), V("sdat"), 1.0, r16),
                    ("tF1", V("tabF", 16, 32), V("tabF", 0, 16), 1024.0), ("tM0", V("tabM", 0, 16), V("tabF", 0, 16), 1.0),
                    ("tM1", V("tabM", 16, 32), V("tabF", 0, 16), 2.0 ** -10), ("init", init, c1("acc", 0), 1.0, k0),
                    ("Fr", V("Fr"), (V("tabF"), hi), 1.0), ("maskJ", pairs("maskJ", 0, C, 0), (V("tabF", 0, 16), lo), ASIDE), ("fib", c1("fib", 0), fi, 1.0),
                    ("Dp", V("Dp"), V("Dn"), -1.0)):
            scaled(*row)
        for k in range(2):
            each(k)
        for b in range(4):
            unpacking(b)
        S["one"] = lambda q: fill("v", V("one"), 1.0)
        S["pad"] = lambda q: fill("v", V("W", xo(0) + 4 * C, xo(R), RX), 0.0)
        S["Z"] = lambda q: op("p", lambda: g.affine_select(T.Z[:], T.nil[:], [[-1, 528]], A.not_equal, 0.5, 3, 4), [V("nil")], [V("Z")])
        S["ip17"] = lambda q: iota(V("ib", 4, 8), [[0, 4]], 0, 17)
        S["ci2"] = lambda q: ts(c1("ci", 2), c1("ib", 4), 4, A.arith_shift_right, 1, A.bitwise_and)
        S["fx"] = lambda q: cp(c1("cols", 10), c1("ci", 2))
        S["i16"] = lambda q: lin(q, c1("cols", 11), fi, 16.0)
        S["LG"] = lambda q: ts(c1("LG", 0), c1("cols", 10), 272.0, A.mult, c1("cols", 11), A.add)
        S["tgu"] = lambda q: (cp(ls28("tgu"), ls28("tgi")), send(ls28("tgu"), ls28("tgl"), "rt"))
        S["trow"] = lambda q: lin(q, V("trow", 0, C), (V("tabI"), ls28("tgl")))
        S["tr0"] = lambda q: fill(q, V("trow", C, C + 16), -256.0)
        S["tk0"] = lambda q: fill(q, V("tk"), 0.0)
        S["ci0"] = lambda q: ts(c1("ci", 0), c1("pint", 0), 15, A.bitwise_and)
        S["ci1"] = lambda q: ts(c1("ci", 1), c1("pint", 0), 4, A.arith_shift_right, 1, A.bitwise_and)
        S["fi"] = lambda q: cp(V("cols", 0, 2), V("ci", 0, 2))
        S["tB0"] = lambda q: ts(V("tabB", 0, 16), V("hh"), fi, A.is_lt, 1024.0, A.add)
        S["tB1"] = lambda q: ts(V("tabB", 16, 32), V("hh"), fi, A.is_lt, 1024.0, A.mult)
        S["tF0"] = lambda q: ts(V("tabF", 0, 16), V("hh"), fi, A.is_equal)
        S["up0"] = lambda q: cp(V("upo", 0, 8), V("h16", 0, 8))
        S["up1"] = lambda q: ts(V("upo", 8, 16), V("h16", 0, 8), 1.0, A.add)
        S["segrow"] = lambda q: act(V("segrow"), V("jj"), AF.Sign)
        S["Hm"] = lambda q: ts(V("Hm"), V("jj"), c1("fib", 0), A.not_equal, 2.0, A.mult)
        S["Qu"] = lambda q: quant(V("uq"), V("us"), V("ut"))
        S["sendW"] = lambda q: (send(V("wq"), V("wl"), "rw", codes=True), send(V("wsc"), V("wls"), "rw"))
        S["hi"] = lambda q: ts(V("hl", 0, 28), ls28("tgi"), 4, A.arith_shift_right)
        S["lo"] = lambda q: ts(V("hl", 28, 56), ls28("tgi"), 15, A.bitwise_and)
        S["hlu"] = lambda q: cp(V("hlu"), V("hl"))
        S["acc"] = lambda q: act(V("seg"), (V("tabB"), hi), AF.Identity, acc=c1("acc", 0))
        S["cum"] = lambda q: scan(V("cum"), V("Fr"), V("Fr"), init, A.add, A.max)
        S["val"] = lambda q: tt(V("val"), (V("tabM"), hi), V("cum"), A.mult)
        S["T1"] = lambda q: turn(V("T1"), V("val"))
        S["seg"] = lambda q: scan(V("seg"), V("segrow"), V("T1"), 0.0, A.mult, A.add)
        S["a0"] = lambda q: cp(ls28("a0"), diag("seg"))
        S["a1"] = lambda q: ts(ls28("a1"), ls28("a0"), 1023, A.bitwise_and)
        S["a2"] = lambda q: ts(ls28("a2"), ls28("a0"), 1008, A.bitwise_and)
        S["a3"] = lambda q: tt(ls28("a3"), ls28("a1"), ls28("s16"), A.add)
        S["a4"] = lambda q: tt(ls28("a0"), ls28("a3"), ls28("a2"), A.add)
        S["spos"] = lambda q: cp(ls28("spos"), ls28("a0"))
        S["ib0"] = lambda q: cp(c1("ib", 0), init)
        S["ib1"] = lambda q: ts(c1("ib", 1), c1("cum", C - 1), 1025.0, A.add)
        S["ob0"] = lambda q: ts(V("ob", 0, 4, 2), V("ib", 0, 2), 1023, A.bitwise_and)
        S["ob1"] = lambda q: ts(V("ob", 1, 4, 2), V("ib", 0, 2), 10, A.arith_shift_right)
        S["se"] = lambda q: cp(V("se", 0, 4), V("ob", 0, 4))
        S["scatter"] = lambda q: scatter(V("swin"), ls28("spos"), V("sdat"))
        S["ST"] = lambda q: turn(V("ST"), V("swin"))
        S["sg"] = lambda q: tt(V("sg"), V("ST", 0, 2 * SL, 32), V("ST", 16, 2 * SL, 32), A.add)
        S["sig"] = lambda q: ts(V("sig"), V("sg"), 2.0, A.mult, ZO + 1022.0, A.add)
        S["Dn"] = lambda q: tt(V("Dn"), (V("maskJ"), V("sig")), V("maskS", XO - 1, XO + SL - 1), A.subtract)
        S["open"] = lambda q: scatter(V("Dn"), V("se", 0, 2), V("big"))

    dma("s", "dtg", T.tgi[:, 0:28], T.tg[:], [], [V("tgi")])
    dma("a", "du", T.ut[:], T.u[:], [], [V("ut")])
    for h, (a, e) in enumerate(halves):
        dma("s", "dx%d" % h, cols(xo(0), a, e)[0], T.x[:, 4 * a:4 * e], [], [cols(xo(0), a, e)])
    dma("s", "dw", T.wq[:].bitcast(dt.uint8), T.wc[:], [], [V("wq")])
    dma("s", "dw", T.wsc[:], T.ws[:], [], [V("wsc")])
    dma("s", "dv", T.vt[:], T.v[:], [], [V("vt")])
    landed("rw", 2 * ne, [V("wl"), V("wls")])
    landed("rt", ne, [V("tgl")])
    for t in range(R):
        landed("re%d" % t, ne, [V("Ll", 16 * t, 16 * t + 16)])
        landed("rl%d" % t, ne, [V("zl%d" % t)])
        landed("rc%d0" % t, 2 * ne, [V("lq%d" % t, 0, HK), V("ls%d" % t)])
        landed("rc%d1" % t, ne, [V("lq%d" % t, HK, K)])

    steps = [{} for _ in range(R + 1)]
    starting(steps[0])
    for t in range(R):
        firing(steps[t], t, RUNS if t else [(0, C)])
        merging(steps[t + 1], t)
    for t, order in enumerate([START] + [ROUND] * (R - 1) + [END]):
        for word in order.split():
            name, q = (word + ":v").split(":")[:2]
            S = steps[t + {"+": 1, "-": -1}.get(name[0], 0)]
            if name.strip("+-") in S:
                S.pop(name.strip("+-"))(q)

    for sem in cnt:
        wait("p", sem, cnt[sem], {})
